import numpy as np
import ml_dtypes


def mxq(x, axis, fmt="e4m3"):
    dtype, down = {"e4m3": (ml_dtypes.float8_e4m3fn, 7), "e5m2": (ml_dtypes.float8_e5m2, 14)}[fmt]
    v = np.moveaxis(np.asarray(x, np.float32).astype(ml_dtypes.bfloat16).astype(np.float64), axis, -1)
    blocks = v.reshape(v.shape[:-1] + (-1, 32))
    amax = np.abs(blocks).max(-1, keepdims=True)
    byte = np.maximum(np.where(amax > 0, np.frexp(amax)[1] - 1 + 127, 0) - down, 1)
    scale = np.exp2(byte - 127.0)
    codes = (blocks / scale).astype(np.float32).astype(dtype).astype(np.float64)
    return np.moveaxis((codes * scale).reshape(v.shape), -1, axis)


WIDE = False


def mx_kscale(k):
    if not WIDE:
        return np.ones(k)
    levels = np.array([10, -10, 5, -5, 0])
    if k % 512:
        return np.exp2(np.random.permutation(np.resize(levels, k // 32))).repeat(32)
    a = np.empty((k // 512, 16))
    for p in range(k // 512):
        a[p, :8] = np.random.permutation(np.resize(levels, 8))
        for g in range(8):
            far = levels[np.abs(levels - a[p, g]) >= 10]
            a[p, g + 8] = far[np.random.randint(len(far))]
    return np.exp2(a.ravel()).repeat(32)


def f64(x):
    return np.asarray(x).astype(np.float64)


def striped(idx):
    return np.tile(idx.reshape(-1, 16).T, (8, 1)).astype(np.uint16)


def unstriped(offs):
    return offs[:16].T.reshape(-1).astype(np.int64)


E2M1 = np.array([0.0, 0.5, 1.0, 1.5, 2.0, 3.0, 4.0, 6.0, -0.0, -0.5, -1.0, -1.5, -2.0, -3.0, -4.0, -6.0])


def pack_weight(w, fmt):
    k, n = w.shape
    w = f64(np.asarray(w, np.float32).astype(ml_dtypes.bfloat16)).reshape(k // 32, 32, n)
    amax = np.abs(w).max(1)
    if fmt == "e4m3":
        byte = np.frexp(amax)[1] - 1 + 127 - 7
    else:
        mant, ex = np.frexp(amax / 6.0)
        byte = np.where(mant > 0.5, ex, ex - 1) + 127
    byte = np.clip(np.where(amax > 0, byte, 1), 1, 254)
    scaled = (w * np.exp2(127.0 - byte)[:, None, :]).reshape(k, n).astype(np.float32)
    by_word = np.ascontiguousarray(scaled.reshape(k // 512, 128, 4, n).transpose(0, 1, 3, 2))
    if fmt == "e4m3":
        words = by_word.astype(ml_dtypes.float8_e4m3fn).view(np.uint8)
    else:
        c = by_word.astype(ml_dtypes.float4_e2m1fn).view(np.uint8) & 0xF
        words = (c[..., 0::2] | (c[..., 1::2] << 4)).reshape(k // 512, 128, 2 * n)
    return np.ascontiguousarray(words), np.ascontiguousarray(byte.astype(np.uint8).reshape(k // 512, 16, n))


def unpack_weight(words, scales, fmt):
    g, _, n = scales.shape
    words = np.ascontiguousarray(words).reshape(g, 128, n, -1)
    if fmt == "e4m3":
        vals = words.view(ml_dtypes.float8_e4m3fn).astype(np.float64)
    else:
        nib = np.empty((g, 128, n, 4), np.uint8)
        nib[..., 0::2] = words & 0xF
        nib[..., 1::2] = words >> 4
        vals = E2M1[nib]
    vals = vals * np.repeat(np.exp2(scales.astype(np.float64) - 127.0), 8, axis=1)[..., None]
    return vals.transpose(0, 1, 3, 2).reshape(g * 512, n)


def gelu(v):
    return 0.5 * v * (1.0 + np.tanh(np.sqrt(2.0 / np.pi) * (v + 0.044715 * v**3)))


K, H, N, T, S = 512, 1024, 256, 2048, 1024

def setup_inputs():
    n = np.random.standard_normal
    s = mx_kscale(K)[:, None]
    u = mx_kscale(H)[:, None]
    tab_words, tab_scales = pack_weight(n((K, T)) * s, "e4m3")
    w4_words, w4_scales = pack_weight(n((H, N)) / np.sqrt(H) / u, "e2m1")
    return {
        "tab_words": tab_words, "tab_scales": tab_scales,
        "offs": striped(np.random.permutation(T)[:S]),
        "wx": (n((K, H)) / np.sqrt(K) / s).astype(np.float32),
        "wy": (n((K, H)) / np.sqrt(K) / s).astype(np.float32),
        "gT": (np.exp(0.5 * n((H, T))) * u).astype(np.float32),
        "w4_words": w4_words, "w4_scales": w4_scales,
    }

def reference(tab_words, tab_scales, offs, wx, wy, gT, w4_words, w4_scales):
    v = unpack_weight(tab_words, tab_scales, "e4m3")[:, unstriped(offs)]
    g = f64(gT)[:, unstriped(offs)]
    dx = mxq(f64(wx), 0, "e4m3").T @ v
    dy = mxq(f64(wy), 0, "e4m3").T @ v
    h = g * np.sqrt(dx * dx + dy * dy)
    w4 = unpack_weight(w4_words, w4_scales, "e2m1")
    return w4.T @ mxq(h, 0, "e4m3")

@@ -1,0 +1,331 @@
+from contextlib import ExitStack
+
+import concourse.mybir as mybir
+from concourse.masks import make_identity
+
+K, H, N, T, S = 512, 1024, 256, 2048, 1024
+FLOPS = 2 * (2 * K * H * S + H * N * S)
+
+F32 = mybir.dt.float32
+BF16 = mybir.dt.bfloat16
+I32 = mybir.dt.int32
+U32 = mybir.dt.uint32
+U16 = mybir.dt.uint16
+U8 = mybir.dt.uint8
+FP8X4 = mybir.dt.float8_e4m3fn_x4
+FP4X4 = mybir.dt.float4_e2m1fn_x4
+ACT = mybir.ActivationFunctionType
+MULT = mybir.AluOpType.mult
+
+P = 128
+PACK = 4
+KP = P * PACK
+PASSES = H // KP
+JT = S // P
+GROUP = 16
+PIECES = (((0,256),(256,512),(512,768),(768,1024)),((0,256),(256,512),(512,768),(768,896),(896,1024)))
+
+
+def tile_list_active_cell_flux_kernel(tc, tab_words, tab_scales, offs, wx, wy, gT, w4_words, w4_scales, out):
+    nc = tc.nc
+    with ExitStack() as ctx:
+        keep = ctx.enter_context(tc.tile_pool(name="keep", bufs=1))
+        psum = ctx.enter_context(tc.psum_pool(name="psum", bufs=1))
+
+        offsets = keep.tile([P, S // GROUP], U16, name="offsets")
+        nc.sync.dma_start(offsets[:], offs)
+
+        def picks(j0, j1):
+            return offsets[:, j0 // GROUP : j1 // GROUP]
+
+        table_scales = keep.tile([P, T // 4], I32, name="table_scales", align_bytes=64)
+        nc.gpsimd.memset(table_scales[:], 0)
+        table_words = keep.tile([P, T], I32, name="table_words", align_bytes=64)
+        w4_codes = keep.tile([P, PASSES, 2 * N], U8, name="w4_codes", align_bytes=64)
+        w4_plane = keep.tile([P, PASSES, N], U8, name="w4_plane", align_bytes=64)
+        weights = {"x": wx, "y": wy}
+        w_raw, g_rows = {}, {}
+
+        def load_scales():
+            scale_rows = tab_scales[0].bitcast(I32)
+            for q in range(4):
+                nc.sync.dma_start(table_scales[32 * q : 32 * q + 4, :], scale_rows[4 * q : 4 * q + 4, :])
+
+        def load_words():
+            nc.sync.dma_start(table_words[:], tab_words[0].rearrange("p t i -> p (t i)").bitcast(I32))
+
+        def load_w(name, a, c0, c1):
+            w_raw[name, a, c0] = keep.tile([P, PACK, c1 - c0], F32, name="raw_%s%d_%d" % (name, a, c0))
+            nc.sync.dma_start(
+                w_raw[name, a, c0][:], weights[name][:, a * KP + c0 : a * KP + c1].rearrange("(p i) c -> p i c", i=PACK)
+            )
+
+        def load_g(a, t):
+            g_rows[a, t] = keep.tile([P, T], F32, name="g%d%d" % (a, t))
+            nc.sync.dma_start(g_rows[a, t][:], gT[a * KP : (a + 1) * KP, :].rearrange("(p t) c -> t p c", t=PACK)[t])
+
+        def load_w4():
+            nc.sync.dma_start(w4_codes[:].bitcast(I32), w4_words.rearrange("a p b -> p a b").bitcast(I32))
+            for q in range(4):
+                nc.sync.dma_start(
+                    w4_plane[32 * q : 32 * q + 4].bitcast(I32),
+                    w4_scales[:, 4 * q : 4 * q + 4, :].rearrange("a r n -> r a n").bitcast(I32),
+                )
+
+        ident_made = keep.tile([P, P], F32, name="ident_made")
+        make_identity(nc, ident_made[:])
+        nc.gpsimd.memset(w4_plane[:], 0)
+        ident = keep.tile([P, P], F32, name="ident")
+        nc.scalar.activation(ident[:], ident_made[:], ACT.Copy)
+
+        load_w("x", 0, 256, 512)
+        load_scales()
+        load_w("x", 0, 0, 256)
+        load_words()
+        load_w("y", 0, 0, 256)
+        load_w("y", 0, 256, 512)
+        load_w("y", 1, 0, 512)
+        load_w("x", 1, 0, 512)
+        load_g(0, 0)
+        load_g(0, 1)
+        load_g(0, 2)
+        load_g(0, 3)
+        load_g(1, 0)
+        load_g(1, 2)
+        load_g(1, 1)
+        load_g(1, 3)
+        load_w4()
+
+        v_words = keep.tile([P, S], I32, name="v_words", align_bytes=64)
+        v_scales = keep.tile([P, S], U8, name="v_scales", align_bytes=64)
+
+        def gather_scales(j0, j1):
+            nc.vector.tensor_copy(v_scales[:, j0:j1], table_scales[:].bitcast(U8).indirect(picks(j0, j1)))
+
+        def gather_words(j0, j1):
+            nc.vector.tensor_copy(v_words[:, j0:j1].bitcast(U32), table_words[:].bitcast(U32).indirect(picks(j0, j1)))
+
+        def interleave(engine, dst, src):
+            d = dst.rearrange("p (c i t) -> p c t i", i=4, t=PACK)
+            s = src.rearrange("p t (c i) -> p c t i", i=4)
+            if engine == "vector":
+                nc.vector.tensor_copy(d, s)
+            else:
+                nc.scalar.activation(d, s, ACT.Copy)
+
+        w_bf, w_codes, w_scales = {}, {}, {}
+        for name in weights:
+            for a in range(PASSES):
+                w_codes[name, a] = keep.tile([P, KP], U32, name="codes_%s%d" % (name, a), align_bytes=64)
+                w_scales[name, a] = keep.tile([P, KP], U8, name="scales_%s%d" % (name, a), align_bytes=64)
+
+        def round_w(name, a, c0, c1, engine="vector"):
+            w_bf[name, a, c0] = keep.tile([P, PACK * (c1 - c0)], BF16, name="w_bf", bufs=2, align_bytes=64)
+            interleave(engine, w_bf[name, a, c0][:], w_raw[name, a, c0][:])
+
+        def quantize_w(name, a, c0, c1):
+            nc.vector.quantize_mx(
+                out=w_codes[name, a][:, c0:c1].bitcast(FP8X4), scales=w_scales[name, a][:, c0:c1], in_=w_bf[name, a, c0][:]
+            )
+
+        squares = {}
+
+        def gradient(name, a, jt):
+            cols = slice(jt * P, (jt + 1) * P)
+            d = psum.tile([P, KP], F32, name="grad", bufs=5)
+            nc.tensor.matmul_mx(
+                out=d[:],
+                lhsT=v_words[:, cols].bitcast(FP8X4),
+                lhsT_scale=v_scales[:, cols],
+                rhs=w_codes[name, a][:].bitcast(FP8X4),
+                rhs_scale=w_scales[name, a][:],
+                start=True,
+                stop=True,
+            )
+            squares[name, a, jt] = keep.tile([P, PACK, P], F32, name="square_" + name, bufs=7 if name == "x" else 3)
+            nc.scalar.activation(squares[name, a, jt][:], d[:].rearrange("j (m t) -> j t m", t=PACK), ACT.Square)
+
+        roots = {}
+
+        def length(a, jt):
+            total = psum.tile([P, PACK, P], F32, name="total", bufs=3)
+            for t in range(PACK):
+                nc.tensor.matmul(total[:, t, :], squares["y", a, jt][:, t, :], ident[:], start=True, stop=False, is_transpose=True)
+                nc.tensor.matmul(total[:, t, :], squares["x", a, jt][:, t, :], ident[:], start=False, stop=True, is_transpose=True)
+            k = [n for n, (j0, j1) in enumerate(PIECES[a]) if j0 <= jt * P < j1][0]
+            j0, j1 = PIECES[a][k]
+            if jt * P == j0:
+                roots[a, k] = keep.tile([P, PACK, j1 - j0], F32, name="root%d_%d" % (a, k))
+            nc.scalar.activation(roots[a, k][:, :, jt * P - j0 : (jt + 1) * P - j0], total[:], ACT.Sqrt)
+
+        h_f32, h_bf = {}, {}
+        h_codes = keep.tile([P, PASSES, S], U32, name="h_codes", align_bytes=64)
+        h_scales = keep.tile([P, PASSES, S], U8, name="h_scales", align_bytes=64)
+
+        def flux(a, k, t):
+            j0, j1 = PIECES[a][k]
+            if (a, k) not in h_f32:
+                h_f32[a, k] = keep.tile([P, PACK, j1 - j0], F32, name="h_f32_%d" % (j1 - j0), bufs={256: 5, 128: 2}[j1 - j0])
+            nc.vector.tensor_tensor(h_f32[a, k][:, t, :], g_rows[a, t][:].indirect(picks(j0, j1)), roots[a, k][:, t, :], MULT)
+
+        def round_h(engine, a, k):
+            j0, j1 = PIECES[a][k]
+            h_bf[a, k] = keep.tile([P, PACK * (j1 - j0)], BF16, name="h_bf", bufs=3, align_bytes=64)
+            interleave(engine, h_bf[a, k][:], h_f32[a, k][:])
+
+        def quantize_h(a, k):
+            j0, j1 = PIECES[a][k]
+            nc.vector.quantize_mx(out=h_codes[:, a, j0:j1].bitcast(FP8X4), scales=h_scales[:, a, j0:j1], in_=h_bf[a, k][:])
+
+        out_v = out.rearrange("(u p) j -> p u j", p=P)
+
+        def project(j0, j1, engines):
+            width = j1 - j0
+            step = KP if width == KP else P
+            staged = keep.tile([P, 2, width], F32, name="staged%d" % j0)
+            for u in range(N // P):
+                acc = psum.tile([P, width], F32, name="grad", bufs=5)
+                for c0 in range(0, width, step):
+                    for a in range(PASSES):
+                        nc.tensor.matmul_mx(
+                            out=acc[:, c0 : c0 + step],
+                            lhsT=w4_codes[:, a, 2 * P * u : 2 * P * (u + 1)].bitcast(FP4X4),
+                            lhsT_scale=w4_plane[:, a, P * u : P * (u + 1)],
+                            rhs=h_codes[:, a, j0 + c0 : j0 + c0 + step].bitcast(FP8X4),
+                            rhs_scale=h_scales[:, a, j0 + c0 : j0 + c0 + step],
+                            start=(a == 0),
+                            stop=(a == PASSES - 1),
+                        )
+                if engines[u] == "s":
+                    nc.scalar.copy(staged[:, u, :], acc[:])
+                else:
+                    nc.vector.tensor_copy(staged[:, u, :], acc[:])
+            nc.sync.dma_start(out_v[:, :, j0:j1], staged[:])
+
+        gather_words(0, 256)
+        round_w("x", 0, 0, 256, "scalar")
+        gather_scales(512, 768)
+        gather_words(512, 768)
+        gather_scales(256, 512)
+        gather_words(256, 512)
+        round_w("x", 0, 256, 512)
+        quantize_w("x", 0, 0, 256)
+        quantize_w("x", 0, 256, 512)
+        gather_scales(0, 256)
+        round_w("y", 0, 256, 512)
+        gradient("x", 0, 3)
+        round_w("y", 0, 0, 256, "scalar")
+        quantize_w("y", 0, 0, 256)
+        gradient("x", 0, 2)
+        gradient("x", 0, 0)
+        gradient("x", 0, 4)
+        quantize_w("y", 0, 256, 512)
+        gradient("y", 0, 0)
+        gradient("x", 0, 1)
+        gradient("y", 0, 2)
+        gather_words(768, 1024)
+        gradient("y", 0, 1)
+        length(0, 0)
+        gradient("y", 0, 3)
+        gradient("x", 0, 5)
+        length(0, 2)
+        length(0, 1)
+        round_w("x", 1, 0, 512)
+        round_w("y", 1, 0, 512)
+        quantize_w("y", 1, 0, 512)
+        flux(0, 0, 0)
+        gather_scales(768, 1024)
+        gradient("y", 0, 4)
+        quantize_w("x", 1, 0, 512)
+        gradient("y", 0, 5)
+        flux(0, 0, 2)
+        length(0, 3)
+        gradient("x", 0, 6)
+        length(0, 4)
+        length(0, 5)
+        flux(0, 2, 2)
+        gradient("y", 0, 6)
+        gradient("x", 0, 7)
+        flux(0, 1, 2)
+        flux(0, 0, 1)
+        gradient("y", 0, 7)
+        flux(0, 1, 1)
+        gradient("x", 1, 0)
+        flux(0, 0, 3)
+        round_h("vector", 0, 0)
+        flux(0, 1, 3)
+        flux(0, 2, 0)
+        gradient("x", 1, 2)
+        quantize_h(0, 0)
+        gradient("x", 1, 1)
+        flux(0, 1, 0)
+        length(0, 6)
+        flux(0, 2, 1)
+        length(0, 7)
+        flux(0, 2, 3)
+        flux(0, 3, 2)
+        flux(0, 3, 3)
+        round_h("vector", 0, 2)
+        flux(0, 3, 1)
+        flux(0, 3, 0)
+        round_h("scalar", 0, 1)
+        round_h("vector", 0, 3)
+        quantize_h(0, 2)
+        gradient("y", 1, 0)
+        gradient("y", 1, 1)
+        length(1, 0)
+        gradient("y", 1, 3)
+        gradient("x", 1, 4)
+        gradient("x", 1, 3)
+        length(1, 1)
+        flux(1, 0, 3)
+        gradient("y", 1, 2)
+        flux(1, 0, 0)
+        flux(1, 0, 1)
+        quantize_h(0, 3)
+        flux(1, 0, 2)
+        length(1, 2)
+        quantize_h(0, 1)
+        gradient("y", 1, 4)
+        round_h("vector", 1, 0)
+        length(1, 3)
+        flux(1, 1, 0)
+        gradient("x", 1, 5)
+        quantize_h(1, 0)
+        flux(1, 1, 2)
+        gradient("y", 1, 6)
+        flux(1, 1, 1)
+        length(1, 4)
+        project(0, 256, "vs")
+        gradient("y", 1, 5)
+        gradient("x", 1, 6)
+        gradient("x", 1, 7)
+        length(1, 6)
+        flux(1, 1, 3)
+        length(1, 5)
+        gradient("y", 1, 7)
+        flux(1, 2, 2)
+        flux(1, 2, 0)
+        flux(1, 2, 3)
+        length(1, 7)
+        flux(1, 2, 1)
+        round_h("scalar", 1, 2)
+        flux(1, 4, 3)
+        flux(1, 4, 2)
+        flux(1, 4, 0)
+        flux(1, 4, 1)
+        flux(1, 3, 1)
+        round_h("scalar", 1, 4)
+        round_h("scalar", 1, 1)
+        flux(1, 3, 0)
+        flux(1, 3, 3)
+        quantize_h(1, 1)
+        quantize_h(1, 4)
+        flux(1, 3, 2)
+        project(256, 512, "sv")
+        quantize_h(1, 2)
+        round_h("scalar", 1, 3)
+        quantize_h(1, 3)
+        project(512, 768, "sv")
+        project(768, 896, "vs")
+        project(896, 1024, "vs")

@@ -23,7 +23,8 @@ KP = P * PACK
 PASSES = H // KP
 JT = S // P
 GROUP = 16
-PIECES = (((0,256),(256,512),(512,768),(768,1024)),((0,256),(256,512),(512,768),(768,896),(896,1024)))
+PIECES = (((0,512),(512,1024)),((0,256),(256,512),(512,768),(768,896),(896,1024)))
+UNITS = ((0,0,1,0),(0,1,1,0),(0,0,1,512),(0,1,1,512),(0,2,1,0),(0,2,1,512),(0,3,1,0),(0,3,1,512),(1,0,2,0),(1,2,2,0),(1,0,2,256),(1,2,2,256),(1,0,2,512),(1,2,2,512),(1,0,4,768),(1,0,4,896))
 
 
 def tile_list_active_cell_flux_kernel(tc, tab_words, tab_scales, offs, wx, wy, gT, w4_words, w4_scales, out):
@@ -72,27 +73,25 @@ def tile_list_active_cell_flux_kernel(tc, tab_words, tab_scales, offs, wx, wy, g
                     w4_scales[:, 4 * q : 4 * q + 4, :].rearrange("a r n -> r a n").bitcast(I32),
                 )
 
-        ident_made = keep.tile([P, P], F32, name="ident_made")
-        make_identity(nc, ident_made[:])
-        nc.gpsimd.memset(w4_plane[:], 0)
         ident = keep.tile([P, P], F32, name="ident")
-        nc.scalar.activation(ident[:], ident_made[:], ACT.Copy)
+        make_identity(nc, ident[:])
+        nc.gpsimd.memset(w4_plane[:], 0)
+        warm = keep.tile([P, 1], F32, name="warm")
+        nc.scalar.activation(warm[:], ident[:, 0:1], ACT.Sqrt)
 
-        load_w("x", 0, 256, 512)
+        load_w("x", 0, 0, 512)
         load_scales()
-        load_w("x", 0, 0, 256)
         load_words()
-        load_w("y", 0, 0, 256)
-        load_w("y", 0, 256, 512)
-        load_w("y", 1, 0, 512)
+        load_w("y", 0, 0, 512)
         load_w("x", 1, 0, 512)
+        load_w("y", 1, 0, 512)
         load_g(0, 0)
         load_g(0, 1)
         load_g(0, 2)
         load_g(0, 3)
         load_g(1, 0)
-        load_g(1, 2)
         load_g(1, 1)
+        load_g(1, 2)
         load_g(1, 3)
         load_w4()
 
@@ -121,52 +120,67 @@ def tile_list_active_cell_flux_kernel(tc, tab_words, tab_scales, offs, wx, wy, g
 
         def round_w(name, a, c0, c1, engine="vector"):
             w_bf[name, a, c0] = keep.tile([P, PACK * (c1 - c0)], BF16, name="w_bf", bufs=2, align_bytes=64)
-            interleave(engine, w_bf[name, a, c0][:], w_raw[name, a, c0][:])
+            d = w_bf[name, a, c0][:].rearrange("p (t m i) -> p m i t", t=PACK, i=PACK)
+            s = w_raw[name, a, c0][:].rearrange("p i (m t) -> p m i t", t=PACK)
+            if engine == "vector":
+                nc.vector.tensor_copy(d, s)
+            else:
+                nc.scalar.activation(d, s, ACT.Copy)
 
         def quantize_w(name, a, c0, c1):
             nc.vector.quantize_mx(
                 out=w_codes[name, a][:, c0:c1].bitcast(FP8X4), scales=w_scales[name, a][:, c0:c1], in_=w_bf[name, a, c0][:]
             )
 
-        squares = {}
-
-        def gradient(name, a, jt):
-            cols = slice(jt * P, (jt + 1) * P)
-            d = psum.tile([P, KP], F32, name="grad", bufs=5)
-            nc.tensor.matmul_mx(
-                out=d[:],
-                lhsT=v_words[:, cols].bitcast(FP8X4),
-                lhsT_scale=v_scales[:, cols],
-                rhs=w_codes[name, a][:].bitcast(FP8X4),
-                rhs_scale=w_scales[name, a][:],
-                start=True,
-                stop=True,
-            )
-            squares[name, a, jt] = keep.tile([P, PACK, P], F32, name="square_" + name, bufs=7 if name == "x" else 3)
-            nc.scalar.activation(squares[name, a, jt][:], d[:].rearrange("j (m t) -> j t m", t=PACK), ACT.Square)
-
-        roots = {}
-
-        def length(a, jt):
-            total = psum.tile([P, PACK, P], F32, name="total", bufs=3)
-            for t in range(PACK):
-                nc.tensor.matmul(total[:, t, :], squares["y", a, jt][:, t, :], ident[:], start=True, stop=False, is_transpose=True)
-                nc.tensor.matmul(total[:, t, :], squares["x", a, jt][:, t, :], ident[:], start=False, stop=True, is_transpose=True)
-            k = [n for n, (j0, j1) in enumerate(PIECES[a]) if j0 <= jt * P < j1][0]
-            j0, j1 = PIECES[a][k]
-            if jt * P == j0:
-                roots[a, k] = keep.tile([P, PACK, j1 - j0], F32, name="root%d_%d" % (a, k))
-            nc.scalar.activation(roots[a, k][:, :, jt * P - j0 : (jt + 1) * P - j0], total[:], ACT.Sqrt)
-
-        h_f32, h_bf = {}, {}
+        squares, roots, h_f32, h_bf = {}, {}, {}, {}
         h_codes = keep.tile([P, PASSES, S], U32, name="h_codes", align_bytes=64)
         h_scales = keep.tile([P, PASSES, S], U8, name="h_scales", align_bytes=64)
 
-        def flux(a, k, t):
-            j0, j1 = PIECES[a][k]
+        def gradient(name, u):
+            a, t0, nt, j0 = UNITS[u]
+            d = psum.tile([P, PACK // nt, nt * P], F32, name="grad", bufs=5)
+            rows = slice(t0 * P, (t0 + nt) * P)
+            for b in range(PACK // nt):
+                cols = slice(j0 + b * P, j0 + (b + 1) * P)
+                nc.tensor.matmul_mx(
+                    out=d[:, b, :],
+                    lhsT=v_words[:, cols].bitcast(FP8X4),
+                    lhsT_scale=v_scales[:, cols],
+                    rhs=w_codes[name, a][:, rows].bitcast(FP8X4),
+                    rhs_scale=w_scales[name, a][:, rows],
+                    start=True,
+                    stop=True,
+                )
+            squares[name, u] = keep.tile([P, PACK // nt, nt * P], F32, name="square_" + name, bufs=6 if name == "x" else 3)
+            nc.scalar.activation(squares[name, u][:], d[:], ACT.Square)
+
+        def length(u):
+            a, t0, nt, j0 = UNITS[u]
+            total = psum.tile([P, nt, KP // nt], F32, name="total", bufs=3)
+            for t in range(nt):
+                for b in range(PACK // nt):
+                    for name in ("y", "x"):
+                        nc.tensor.matmul(
+                            total[:, t, b * P : (b + 1) * P],
+                            squares[name, u][:, b, t * P : (t + 1) * P],
+                            ident[:],
+                            start=(name == "y"),
+                            stop=(name == "x"),
+                            is_transpose=True,
+                        )
+            roots[u] = keep.tile([P, nt, KP // nt], F32, name="root", bufs=8)
+            nc.scalar.activation(roots[u][:], total[:], ACT.Sqrt)
+
+        def flux(u):
+            a, t0, nt, j0 = UNITS[u]
+            width = KP // nt
+            k = [n for n, pc in enumerate(PIECES[a]) if pc[0] == j0][0]
             if (a, k) not in h_f32:
-                h_f32[a, k] = keep.tile([P, PACK, j1 - j0], F32, name="h_f32_%d" % (j1 - j0), bufs={256: 5, 128: 2}[j1 - j0])
-            nc.vector.tensor_tensor(h_f32[a, k][:, t, :], g_rows[a, t][:].indirect(picks(j0, j1)), roots[a, k][:, t, :], MULT)
+                h_f32[a, k] = keep.tile([P, PACK, width], F32, name="h_f32_%d_%d" % (a, k))
+            for t in range(nt):
+                nc.vector.tensor_tensor(
+                    h_f32[a, k][:, t0 + t, :], g_rows[a, t0 + t][:].indirect(picks(j0, j0 + width)), roots[u][:, t, :], MULT
+                )
 
         def round_h(engine, a, k):
             j0, j1 = PIECES[a][k]
@@ -202,130 +216,99 @@ def tile_list_active_cell_flux_kernel(tc, tab_words, tab_scales, offs, wx, wy, g
                     nc.vector.tensor_copy(staged[:, u, :], acc[:])
             nc.sync.dma_start(out_v[:, :, j0:j1], staged[:])
 
-        gather_words(0, 256)
-        round_w("x", 0, 0, 256, "scalar")
+        round_w("x", 0, 0, 512)
+        gather_scales(0, 512)
+        quantize_w("x", 0, 0, 512)
+        gather_words(0, 512)
+        gradient("x", 0)
+        gradient("x", 1)
         gather_scales(512, 768)
-        gather_words(512, 768)
-        gather_scales(256, 512)
-        gather_words(256, 512)
-        round_w("x", 0, 256, 512)
-        quantize_w("x", 0, 0, 256)
-        quantize_w("x", 0, 256, 512)
-        gather_scales(0, 256)
-        round_w("y", 0, 256, 512)
-        gradient("x", 0, 3)
-        round_w("y", 0, 0, 256, "scalar")
-        quantize_w("y", 0, 0, 256)
-        gradient("x", 0, 2)
-        gradient("x", 0, 0)
-        gradient("x", 0, 4)
-        quantize_w("y", 0, 256, 512)
-        gradient("y", 0, 0)
-        gradient("x", 0, 1)
-        gradient("y", 0, 2)
-        gather_words(768, 1024)
-        gradient("y", 0, 1)
-        length(0, 0)
-        gradient("y", 0, 3)
-        gradient("x", 0, 5)
-        length(0, 2)
-        length(0, 1)
-        round_w("x", 1, 0, 512)
-        round_w("y", 1, 0, 512)
-        quantize_w("y", 1, 0, 512)
-        flux(0, 0, 0)
+        round_w("y", 0, 0, 512)
         gather_scales(768, 1024)
-        gradient("y", 0, 4)
+        quantize_w("y", 0, 0, 512)
+        gradient("x", 4)
+        gradient("x", 6)
+        gather_words(512, 1024)
+        gradient("y", 0)
+        gradient("y", 1)
+        round_w("x", 1, 0, 512)
+        gradient("x", 2)
+        length(0)
+        gradient("y", 2)
         quantize_w("x", 1, 0, 512)
-        gradient("y", 0, 5)
-        flux(0, 0, 2)
-        length(0, 3)
-        gradient("x", 0, 6)
-        length(0, 4)
-        length(0, 5)
-        flux(0, 2, 2)
-        gradient("y", 0, 6)
-        gradient("x", 0, 7)
-        flux(0, 1, 2)
-        flux(0, 0, 1)
-        gradient("y", 0, 7)
-        flux(0, 1, 1)
-        gradient("x", 1, 0)
-        flux(0, 0, 3)
+        round_w("y", 1, 0, 512)
+        length(1)
+        gradient("x", 3)
+        gradient("y", 3)
+        length(2)
+        quantize_w("y", 1, 0, 512)
+        flux(0)
+        gradient("y", 4)
+        gradient("x", 5)
+        length(3)
+        flux(1)
+        gradient("y", 5)
+        length(4)
+        flux(2)
+        gradient("y", 6)
+        gradient("x", 7)
+        length(5)
+        flux(3)
+        gradient("y", 7)
+        gradient("x", 8)
+        length(6)
+        flux(4)
+        gradient("y", 8)
+        gradient("x", 9)
+        length(7)
+        flux(5)
+        flux(6)
+        gradient("y", 9)
+        gradient("x", 10)
+        length(8)
         round_h("vector", 0, 0)
-        flux(0, 1, 3)
-        flux(0, 2, 0)
-        gradient("x", 1, 2)
+        flux(7)
         quantize_h(0, 0)
-        gradient("x", 1, 1)
-        flux(0, 1, 0)
-        length(0, 6)
-        flux(0, 2, 1)
-        length(0, 7)
-        flux(0, 2, 3)
-        flux(0, 3, 2)
-        flux(0, 3, 3)
-        round_h("vector", 0, 2)
-        flux(0, 3, 1)
-        flux(0, 3, 0)
-        round_h("scalar", 0, 1)
-        round_h("vector", 0, 3)
-        quantize_h(0, 2)
-        gradient("y", 1, 0)
-        gradient("y", 1, 1)
-        length(1, 0)
-        gradient("y", 1, 3)
-        gradient("x", 1, 4)
-        gradient("x", 1, 3)
-        length(1, 1)
-        flux(1, 0, 3)
-        gradient("y", 1, 2)
-        flux(1, 0, 0)
-        flux(1, 0, 1)
-        quantize_h(0, 3)
-        flux(1, 0, 2)
-        length(1, 2)
+        gradient("y", 10)
+        gradient("x", 11)
+        length(9)
+        round_h("vector", 0, 1)
+        flux(8)
         quantize_h(0, 1)
-        gradient("y", 1, 4)
+        flux(9)
+        gradient("y", 11)
+        gradient("x", 12)
+        length(10)
         round_h("vector", 1, 0)
-        length(1, 3)
-        flux(1, 1, 0)
-        gradient("x", 1, 5)
+        flux(10)
         quantize_h(1, 0)
-        flux(1, 1, 2)
-        gradient("y", 1, 6)
-        flux(1, 1, 1)
-        length(1, 4)
-        project(0, 256, "vs")
-        gradient("y", 1, 5)
-        gradient("x", 1, 6)
-        gradient("x", 1, 7)
-        length(1, 6)
-        flux(1, 1, 3)
-        length(1, 5)
-        gradient("y", 1, 7)
-        flux(1, 2, 2)
-        flux(1, 2, 0)
-        flux(1, 2, 3)
-        length(1, 7)
-        flux(1, 2, 1)
-        round_h("scalar", 1, 2)
-        flux(1, 4, 3)
-        flux(1, 4, 2)
-        flux(1, 4, 0)
-        flux(1, 4, 1)
-        flux(1, 3, 1)
-        round_h("scalar", 1, 4)
+        gradient("y", 12)
+        gradient("x", 13)
+        length(11)
+        flux(11)
+        gradient("y", 13)
+        gradient("x", 14)
+        length(12)
+        gradient("y", 14)
+        gradient("x", 15)
+        length(13)
+        gradient("y", 15)
+        length(14)
+        length(15)
+        project(0, 256, "ss")
+        flux(12)
         round_h("scalar", 1, 1)
-        flux(1, 3, 0)
-        flux(1, 3, 3)
+        flux(13)
         quantize_h(1, 1)
-        quantize_h(1, 4)
-        flux(1, 3, 2)
-        project(256, 512, "sv")
+        round_h("scalar", 1, 2)
+        flux(14)
+        project(256, 512, "ss")
         quantize_h(1, 2)
+        flux(15)
         round_h("scalar", 1, 3)
+        round_h("vector", 1, 4)
+        project(512, 768, "ss")
         quantize_h(1, 3)
-        project(512, 768, "sv")
-        project(768, 896, "vs")
+        quantize_h(1, 4)
+        project(768, 896, "sv")
         project(896, 1024, "vs")

@@ -24,7 +24,7 @@ PASSES = H // KP
 JT = S // P
 GROUP = 16
 PIECES = (((0,512),(512,1024)),((0,256),(256,512),(512,768),(768,896),(896,1024)))
-UNITS = ((0,0,1,0),(0,1,1,0),(0,0,1,512),(0,1,1,512),(0,2,1,0),(0,2,1,512),(0,3,1,0),(0,3,1,512),(1,0,2,0),(1,2,2,0),(1,0,2,256),(1,2,2,256),(1,0,2,512),(1,2,2,512),(1,0,4,768),(1,0,4,896))
+UNITS = ((0,0,1,0),(0,0,1,512),(0,1,1,0),(0,1,1,512),(0,2,1,0),(0,2,1,512),(0,3,1,0),(0,3,1,512),(1,0,2,0),(1,0,2,256),(1,2,2,0),(1,2,2,256),(1,0,2,512),(1,2,2,512),(1,0,4,768),(1,0,4,896))
 
 
 def tile_list_active_cell_flux_kernel(tc, tab_words, tab_scales, offs, wx, wy, gT, w4_words, w4_scales, out):
@@ -48,9 +48,9 @@ def tile_list_active_cell_flux_kernel(tc, tab_words, tab_scales, offs, wx, wy, g
         w_raw, g_rows = {}, {}
 
         def load_scales():
-            scale_rows = tab_scales[0].bitcast(I32)
-            for q in range(4):
-                nc.sync.dma_start(table_scales[32 * q : 32 * q + 4, :], scale_rows[4 * q : 4 * q + 4, :])
+            scale_rows = tab_scales[0].bitcast(I32).rearrange("(q r) c -> r q c", r=4)
+            for r in range(4):
+                nc.sync.dma_start(table_scales[r:P:32, :], scale_rows[r])
 
         def load_words():
             nc.sync.dma_start(table_words[:], tab_words[0].rearrange("p t i -> p (t i)").bitcast(I32))
@@ -171,16 +171,15 @@ def tile_list_active_cell_flux_kernel(tc, tab_words, tab_scales, offs, wx, wy, g
             roots[u] = keep.tile([P, nt, KP // nt], F32, name="root", bufs=8)
             nc.scalar.activation(roots[u][:], total[:], ACT.Sqrt)
 
-        def flux(u):
+        def flux(u, t):
             a, t0, nt, j0 = UNITS[u]
             width = KP // nt
             k = [n for n, pc in enumerate(PIECES[a]) if pc[0] == j0][0]
             if (a, k) not in h_f32:
                 h_f32[a, k] = keep.tile([P, PACK, width], F32, name="h_f32_%d_%d" % (a, k))
-            for t in range(nt):
-                nc.vector.tensor_tensor(
-                    h_f32[a, k][:, t0 + t, :], g_rows[a, t0 + t][:].indirect(picks(j0, j0 + width)), roots[u][:, t, :], MULT
-                )
+            nc.vector.tensor_tensor(
+                h_f32[a, k][:, t0 + t, :], g_rows[a, t0 + t][:].indirect(picks(j0, j0 + width)), roots[u][:, t, :], MULT
+            )
 
         def round_h(engine, a, k):
             j0, j1 = PIECES[a][k]
@@ -216,99 +215,109 @@ def tile_list_active_cell_flux_kernel(tc, tab_words, tab_scales, offs, wx, wy, g
                     nc.vector.tensor_copy(staged[:, u, :], acc[:])
             nc.sync.dma_start(out_v[:, :, j0:j1], staged[:])
 
-        round_w("x", 0, 0, 512)
+        round_w("x", 0, 0, 512, "scalar")
         gather_scales(0, 512)
+        gather_scales(512, 1024)
         quantize_w("x", 0, 0, 512)
         gather_words(0, 512)
         gradient("x", 0)
-        gradient("x", 1)
-        gather_scales(512, 768)
+        gradient("x", 2)
         round_w("y", 0, 0, 512)
-        gather_scales(768, 1024)
-        quantize_w("y", 0, 0, 512)
         gradient("x", 4)
         gradient("x", 6)
         gather_words(512, 1024)
+        quantize_w("y", 0, 0, 512)
+        gradient("x", 1)
         gradient("y", 0)
-        gradient("y", 1)
         round_w("x", 1, 0, 512)
-        gradient("x", 2)
-        length(0)
-        gradient("y", 2)
-        quantize_w("x", 1, 0, 512)
+        gradient("y", 1)
         round_w("y", 1, 0, 512)
+        gradient("y", 2)
+        length(0)
         length(1)
+        quantize_w("x", 1, 0, 512)
+        quantize_w("y", 1, 0, 512)
         gradient("x", 3)
         gradient("y", 3)
         length(2)
-        quantize_w("y", 1, 0, 512)
-        flux(0)
+        flux(0, 0)
         gradient("y", 4)
-        gradient("x", 5)
         length(3)
-        flux(1)
+        flux(1, 0)
+        gradient("x", 5)
         gradient("y", 5)
         length(4)
-        flux(2)
+        flux(2, 0)
         gradient("y", 6)
-        gradient("x", 7)
         length(5)
-        flux(3)
+        flux(3, 0)
+        gradient("x", 7)
         gradient("y", 7)
-        gradient("x", 8)
         length(6)
-        flux(4)
+        flux(4, 0)
+        gradient("x", 8)
         gradient("y", 8)
-        gradient("x", 9)
         length(7)
-        flux(5)
-        flux(6)
+        flux(5, 0)
+        flux(6, 0)
+        gradient("x", 9)
         gradient("y", 9)
-        gradient("x", 10)
         length(8)
         round_h("vector", 0, 0)
-        flux(7)
+        flux(7, 0)
         quantize_h(0, 0)
-        gradient("y", 10)
-        gradient("x", 11)
-        length(9)
         round_h("vector", 0, 1)
-        flux(8)
+        gradient("x", 10)
+        gradient("y", 10)
+        length(9)
+        flux(8, 0)
         quantize_h(0, 1)
-        flux(9)
+        flux(8, 1)
+        gradient("x", 11)
         gradient("y", 11)
-        gradient("x", 12)
         length(10)
-        round_h("vector", 1, 0)
-        flux(10)
-        quantize_h(1, 0)
+        flux(9, 0)
+        flux(9, 1)
+        gradient("x", 12)
         gradient("y", 12)
-        gradient("x", 13)
         length(11)
-        flux(11)
+        flux(10, 0)
+        flux(10, 1)
+        gradient("x", 13)
         gradient("y", 13)
-        gradient("x", 14)
         length(12)
+        flux(11, 0)
+        round_h("vector", 1, 0)
+        flux(11, 1)
+        quantize_h(1, 0)
+        gradient("x", 14)
         gradient("y", 14)
-        gradient("x", 15)
         length(13)
+        gradient("x", 15)
         gradient("y", 15)
         length(14)
         length(15)
-        project(0, 256, "ss")
-        flux(12)
+        flux(12, 0)
+        flux(12, 1)
         round_h("scalar", 1, 1)
-        flux(13)
+        flux(13, 0)
+        flux(13, 1)
         quantize_h(1, 1)
         round_h("scalar", 1, 2)
-        flux(14)
-        project(256, 512, "ss")
+        flux(14, 0)
+        flux(14, 1)
+        flux(14, 2)
+        flux(14, 3)
+        project(0, 512, "ss")
+        flux(15, 0)
         quantize_h(1, 2)
-        flux(15)
-        round_h("scalar", 1, 3)
-        round_h("vector", 1, 4)
-        project(512, 768, "ss")
+        round_h("vector", 1, 3)
+        flux(15, 1)
+        flux(15, 2)
         quantize_h(1, 3)
+        flux(15, 3)
+        project(512, 768, "ss")
+        round_h("vector", 1, 4)
+        project(768, 896, "ss")
         quantize_h(1, 4)
-        project(768, 896, "sv")
         project(896, 1024, "vs")

@@ -19,84 +19,84 @@ MULT = mybir.AluOpType.mult
 
 P = 128
 PACK = 4
-KP = P * PACK
-PASSES = H // KP
-JT = S // P
-GROUP = 16
-PIECES = (((0,512),(512,1024)),((0,256),(256,512),(512,768),(768,896),(896,1024)))
-UNITS = ((0,0,1,0),(0,0,1,512),(0,1,1,0),(0,1,1,512),(0,2,1,0),(0,2,1,512),(0,3,1,0),(0,3,1,512),(1,0,2,0),(1,0,2,256),(1,2,2,0),(1,2,2,256),(1,0,2,512),(1,2,2,512),(1,0,4,768),(1,0,4,896))
+BANK = P * PACK
+PASSES = H // BANK
+LIST_ROWS = 16
+QUAD = 32
+SCALE_ROWS = 4
+LINE = 4
+
+PIECES = (((0, 512), (512, 1024)), ((0, 512), (512, 768), (768, 896), (896, 1024)))
+
+UNITS = (
+    [(0, t, 1, j0) for t in range(PACK) for j0, j1 in PIECES[0]]
+    + [(1, t, 1, 0) for t in range(PACK)]
+    + [(1, 0, 2, 512), (1, 2, 2, 512), (1, 0, 4, 768), (1, 0, 4, 896)]
+)
+EARLY_DX = (0, 2, 4, 6, 1)
+
+GRAD_BANKS, SUM_BANKS = 4, 4
+DX_BUFS = len(EARLY_DX) + 1
+DY_BUFS = 3
+ROOT_BUFS = 8
+H_BF16_BUFS = 4
 
 
 def tile_list_active_cell_flux_kernel(tc, tab_words, tab_scales, offs, wx, wy, gT, w4_words, w4_scales, out):
     nc = tc.nc
     with ExitStack() as ctx:
-        keep = ctx.enter_context(tc.tile_pool(name="keep", bufs=1))
+        sbuf = ctx.enter_context(tc.tile_pool(name="sbuf", bufs=1))
         psum = ctx.enter_context(tc.psum_pool(name="psum", bufs=1))
 
-        offsets = keep.tile([P, S // GROUP], U16, name="offsets")
+        offsets = sbuf.tile([P, S // LIST_ROWS], U16, name="offsets")
         nc.sync.dma_start(offsets[:], offs)
 
         def picks(j0, j1):
-            return offsets[:, j0 // GROUP : j1 // GROUP]
+            return offsets[:, j0 // LIST_ROWS : j1 // LIST_ROWS]
 
-        table_scales = keep.tile([P, T // 4], I32, name="table_scales", align_bytes=64)
+        table_scales = sbuf.tile([P, T // 4], I32, name="table_scales", align_bytes=64)
         nc.gpsimd.memset(table_scales[:], 0)
-        table_words = keep.tile([P, T], I32, name="table_words", align_bytes=64)
-        w4_codes = keep.tile([P, PASSES, 2 * N], U8, name="w4_codes", align_bytes=64)
-        w4_plane = keep.tile([P, PASSES, N], U8, name="w4_plane", align_bytes=64)
+        table_words = sbuf.tile([P, T], I32, name="table_words", align_bytes=64)
+        w4_codes = sbuf.tile([P, PASSES, 2 * N], U8, name="w4_codes", align_bytes=64)
+        w4_scale_tile = sbuf.tile([P, PASSES, N], U8, name="w4_scale_tile", align_bytes=64)
+        ident = sbuf.tile([P, P], F32, name="ident")
+        make_identity(nc, ident[:])
+        nc.gpsimd.memset(w4_scale_tile[:], 0)
+        warm = sbuf.tile([P, 1], F32, name="warm")
+        nc.scalar.activation(warm[:], ident[:, 0:1], ACT.Sqrt)
+
         weights = {"x": wx, "y": wy}
         w_raw, g_rows = {}, {}
 
-        def load_scales():
-            scale_rows = tab_scales[0].bitcast(I32).rearrange("(q r) c -> r q c", r=4)
-            for r in range(4):
-                nc.sync.dma_start(table_scales[r:P:32, :], scale_rows[r])
-
-        def load_words():
-            nc.sync.dma_start(table_words[:], tab_words[0].rearrange("p t i -> p (t i)").bitcast(I32))
-
-        def load_w(name, a, c0, c1):
-            w_raw[name, a, c0] = keep.tile([P, PACK, c1 - c0], F32, name="raw_%s%d_%d" % (name, a, c0))
+        def load_w(name, a):
+            w_raw[name, a] = sbuf.tile([P, PACK, BANK], F32, name="raw_%s%d" % (name, a))
             nc.sync.dma_start(
-                w_raw[name, a, c0][:], weights[name][:, a * KP + c0 : a * KP + c1].rearrange("(p i) c -> p i c", i=PACK)
+                w_raw[name, a][:], weights[name][:, a * BANK : (a + 1) * BANK].rearrange("(p i) c -> p i c", i=PACK)
             )
 
-        def load_g(a, t):
-            g_rows[a, t] = keep.tile([P, T], F32, name="g%d%d" % (a, t))
-            nc.sync.dma_start(g_rows[a, t][:], gT[a * KP : (a + 1) * KP, :].rearrange("(p t) c -> t p c", t=PACK)[t])
-
-        def load_w4():
-            nc.sync.dma_start(w4_codes[:].bitcast(I32), w4_words.rearrange("a p b -> p a b").bitcast(I32))
-            for q in range(4):
+        load_w("x", 0)
+        scale_rows = tab_scales[0].bitcast(I32).rearrange("(q r) c -> r q c", r=SCALE_ROWS)
+        for r in range(SCALE_ROWS):
+            nc.sync.dma_start(table_scales[r:P:QUAD, :], scale_rows[r])
+        nc.sync.dma_start(table_words[:], tab_words[0].rearrange("p t i -> p (t i)").bitcast(I32))
+        load_w("y", 0)
+        load_w("x", 1)
+        load_w("y", 1)
+        for a in range(PASSES):
+            for t in range(PACK):
+                g_rows[a, t] = sbuf.tile([P, T], F32, name="g%d%d" % (a, t))
                 nc.sync.dma_start(
-                    w4_plane[32 * q : 32 * q + 4].bitcast(I32),
-                    w4_scales[:, 4 * q : 4 * q + 4, :].rearrange("a r n -> r a n").bitcast(I32),
+                    g_rows[a, t][:], gT[a * BANK : (a + 1) * BANK, :].rearrange("(p t) c -> t p c", t=PACK)[t]
                 )
+        nc.sync.dma_start(w4_codes[:].bitcast(I32), w4_words.rearrange("a p b -> p a b").bitcast(I32))
+        for q in range(P // QUAD):
+            nc.sync.dma_start(
+                w4_scale_tile[QUAD * q : QUAD * q + SCALE_ROWS].bitcast(I32),
+                w4_scales[:, SCALE_ROWS * q : SCALE_ROWS * (q + 1), :].rearrange("a r n -> r a n").bitcast(I32),
+            )
 
-        ident = keep.tile([P, P], F32, name="ident")
-        make_identity(nc, ident[:])
-        nc.gpsimd.memset(w4_plane[:], 0)
-        warm = keep.tile([P, 1], F32, name="warm")
-        nc.scalar.activation(warm[:], ident[:, 0:1], ACT.Sqrt)
-
-        load_w("x", 0, 0, 512)
-        load_scales()
-        load_words()
-        load_w("y", 0, 0, 512)
-        load_w("x", 1, 0, 512)
-        load_w("y", 1, 0, 512)
-        load_g(0, 0)
-        load_g(0, 1)
-        load_g(0, 2)
-        load_g(0, 3)
-        load_g(1, 0)
-        load_g(1, 1)
-        load_g(1, 2)
-        load_g(1, 3)
-        load_w4()
-
-        v_words = keep.tile([P, S], I32, name="v_words", align_bytes=64)
-        v_scales = keep.tile([P, S], U8, name="v_scales", align_bytes=64)
+        v_words = sbuf.tile([P, S], I32, name="v_words", align_bytes=64)
+        v_scales = sbuf.tile([P, S], U8, name="v_scales", align_bytes=64)
 
         def gather_scales(j0, j1):
             nc.vector.tensor_copy(v_scales[:, j0:j1], table_scales[:].bitcast(U8).indirect(picks(j0, j1)))
@@ -104,61 +104,60 @@ def tile_list_active_cell_flux_kernel(tc, tab_words, tab_scales, offs, wx, wy, g
         def gather_words(j0, j1):
             nc.vector.tensor_copy(v_words[:, j0:j1].bitcast(U32), table_words[:].bitcast(U32).indirect(picks(j0, j1)))
 
-        def interleave(engine, dst, src):
-            d = dst.rearrange("p (c i t) -> p c t i", i=4, t=PACK)
-            s = src.rearrange("p t (c i) -> p c t i", i=4)
+        def round_copy(engine, dst, src):
             if engine == "vector":
-                nc.vector.tensor_copy(d, s)
+                nc.vector.tensor_copy(dst, src)
             else:
-                nc.scalar.activation(d, s, ACT.Copy)
+                nc.scalar.activation(dst, src, ACT.Copy)
 
-        w_bf, w_codes, w_scales = {}, {}, {}
+        w_bf16, w_codes, w_scales = {}, {}, {}
         for name in weights:
             for a in range(PASSES):
-                w_codes[name, a] = keep.tile([P, KP], U32, name="codes_%s%d" % (name, a), align_bytes=64)
-                w_scales[name, a] = keep.tile([P, KP], U8, name="scales_%s%d" % (name, a), align_bytes=64)
+                w_codes[name, a] = sbuf.tile([P, BANK], U32, name="codes_%s%d" % (name, a), align_bytes=64)
+                w_scales[name, a] = sbuf.tile([P, BANK], U8, name="scales_%s%d" % (name, a), align_bytes=64)
 
-        def round_w(name, a, c0, c1, engine="vector"):
-            w_bf[name, a, c0] = keep.tile([P, PACK * (c1 - c0)], BF16, name="w_bf", bufs=2, align_bytes=64)
-            d = w_bf[name, a, c0][:].rearrange("p (t m i) -> p m i t", t=PACK, i=PACK)
-            s = w_raw[name, a, c0][:].rearrange("p i (m t) -> p m i t", t=PACK)
-            if engine == "vector":
-                nc.vector.tensor_copy(d, s)
-            else:
-                nc.scalar.activation(d, s, ACT.Copy)
-
-        def quantize_w(name, a, c0, c1):
-            nc.vector.quantize_mx(
-                out=w_codes[name, a][:, c0:c1].bitcast(FP8X4), scales=w_scales[name, a][:, c0:c1], in_=w_bf[name, a, c0][:]
+        def round_w(engine, name, a):
+            w_bf16[name, a] = sbuf.tile([P, PACK * BANK], BF16, name="w_bf16", bufs=2, align_bytes=64)
+            round_copy(
+                engine,
+                w_bf16[name, a][:].rearrange("p (t m i) -> p m i t", t=PACK, i=PACK),
+                w_raw[name, a][:].rearrange("p i (m t) -> p m i t", t=PACK),
             )
 
-        squares, roots, h_f32, h_bf = {}, {}, {}, {}
-        h_codes = keep.tile([P, PASSES, S], U32, name="h_codes", align_bytes=64)
-        h_scales = keep.tile([P, PASSES, S], U8, name="h_scales", align_bytes=64)
+        def quantize_w(name, a):
+            nc.vector.quantize_mx(
+                out=w_codes[name, a][:].bitcast(FP8X4), scales=w_scales[name, a][:], in_=w_bf16[name, a][:]
+            )
 
-        def gradient(name, u):
-            a, t0, nt, j0 = UNITS[u]
-            d = psum.tile([P, PACK // nt, nt * P], F32, name="grad", bufs=5)
-            rows = slice(t0 * P, (t0 + nt) * P)
-            for b in range(PACK // nt):
-                cols = slice(j0 + b * P, j0 + (b + 1) * P)
+        squares, roots, h_f32, h_bf16 = {}, {}, {}, {}
+        h_codes = sbuf.tile([P, PASSES, S], U32, name="h_codes", align_bytes=64)
+        h_scales = sbuf.tile([P, PASSES, S], U8, name="h_scales", align_bytes=64)
+
+        def square(name, u):
+            a, t0, planes, j0 = UNITS[u]
+            grad = psum.tile([P, PACK // planes, planes * P], F32, name="grad", bufs=GRAD_BANKS)
+            rows = slice(t0 * P, (t0 + planes) * P)
+            for b in range(PACK // planes):
+                cells = slice(j0 + b * P, j0 + (b + 1) * P)
                 nc.tensor.matmul_mx(
-                    out=d[:, b, :],
-                    lhsT=v_words[:, cols].bitcast(FP8X4),
-                    lhsT_scale=v_scales[:, cols],
+                    out=grad[:, b, :],
+                    lhsT=v_words[:, cells].bitcast(FP8X4),
+                    lhsT_scale=v_scales[:, cells],
                     rhs=w_codes[name, a][:, rows].bitcast(FP8X4),
                     rhs_scale=w_scales[name, a][:, rows],
                     start=True,
                     stop=True,
                 )
-            squares[name, u] = keep.tile([P, PACK // nt, nt * P], F32, name="square_" + name, bufs=6 if name == "x" else 3)
-            nc.scalar.activation(squares[name, u][:], d[:], ACT.Square)
+            squares[name, u] = sbuf.tile(
+                [P, PACK // planes, planes * P], F32, name="square_" + name, bufs=DX_BUFS if name == "x" else DY_BUFS
+            )
+            nc.scalar.activation(squares[name, u][:], grad[:], ACT.Square)
 
-        def length(u):
-            a, t0, nt, j0 = UNITS[u]
-            total = psum.tile([P, nt, KP // nt], F32, name="total", bufs=3)
-            for t in range(nt):
-                for b in range(PACK // nt):
+        def root(u):
+            a, t0, planes, j0 = UNITS[u]
+            total = psum.tile([P, planes, BANK // planes], F32, name="total", bufs=SUM_BANKS)
+            for t in range(planes):
+                for b in range(PACK // planes):
                     for name in ("y", "x"):
                         nc.tensor.matmul(
                             total[:, t, b * P : (b + 1) * P],
@@ -168,156 +167,113 @@ def tile_list_active_cell_flux_kernel(tc, tab_words, tab_scales, offs, wx, wy, g
                             stop=(name == "x"),
                             is_transpose=True,
                         )
-            roots[u] = keep.tile([P, nt, KP // nt], F32, name="root", bufs=8)
+            roots[u] = sbuf.tile([P, planes, BANK // planes], F32, name="root", bufs=ROOT_BUFS)
             nc.scalar.activation(roots[u][:], total[:], ACT.Sqrt)
 
-        def flux(u, t):
-            a, t0, nt, j0 = UNITS[u]
-            width = KP // nt
-            k = [n for n, pc in enumerate(PIECES[a]) if pc[0] == j0][0]
-            if (a, k) not in h_f32:
-                h_f32[a, k] = keep.tile([P, PACK, width], F32, name="h_f32_%d_%d" % (a, k))
-            nc.vector.tensor_tensor(
-                h_f32[a, k][:, t0 + t, :], g_rows[a, t0 + t][:].indirect(picks(j0, j0 + width)), roots[u][:, t, :], MULT
+        def flux(u):
+            a, t0, planes, j0 = UNITS[u]
+            width = BANK // planes
+            piece = PIECES[a].index((j0, j0 + width))
+            if t0 == 0:
+                h_f32[a, piece] = sbuf.tile([P, PACK, width], F32, name="h_f32_%d_%d" % (a, piece))
+            for t in range(planes):
+                nc.vector.tensor_tensor(
+                    h_f32[a, piece][:, t0 + t, :],
+                    g_rows[a, t0 + t][:].indirect(picks(j0, j0 + width)),
+                    roots[u][:, t, :],
+                    MULT,
+                )
+
+        def round_h(engine, a, piece):
+            j0, j1 = PIECES[a][piece]
+            h_bf16[a, piece] = sbuf.tile([P, PACK * (j1 - j0)], BF16, name="h_bf16", bufs=H_BF16_BUFS, align_bytes=64)
+            round_copy(
+                engine,
+                h_bf16[a, piece][:].rearrange("p (c i t) -> p c t i", i=LINE, t=PACK),
+                h_f32[a, piece][:].rearrange("p t (c i) -> p c t i", i=LINE),
             )
 
-        def round_h(engine, a, k):
-            j0, j1 = PIECES[a][k]
-            h_bf[a, k] = keep.tile([P, PACK * (j1 - j0)], BF16, name="h_bf", bufs=3, align_bytes=64)
-            interleave(engine, h_bf[a, k][:], h_f32[a, k][:])
+        def quantize_h(a, piece):
+            j0, j1 = PIECES[a][piece]
+            nc.vector.quantize_mx(
+                out=h_codes[:, a, j0:j1].bitcast(FP8X4), scales=h_scales[:, a, j0:j1], in_=h_bf16[a, piece][:]
+            )
 
-        def quantize_h(a, k):
-            j0, j1 = PIECES[a][k]
-            nc.vector.quantize_mx(out=h_codes[:, a, j0:j1].bitcast(FP8X4), scales=h_scales[:, a, j0:j1], in_=h_bf[a, k][:])
+        out_rows = out.rearrange("(u p) j -> p u j", p=P)
 
-        out_v = out.rearrange("(u p) j -> p u j", p=P)
-
-        def project(j0, j1, engines):
+        def project(piece, first_engine):
+            j0, j1 = PIECES[1][piece]
             width = j1 - j0
-            step = KP if width == KP else P
-            staged = keep.tile([P, 2, width], F32, name="staged%d" % j0)
+            step = BANK if width == BANK else P
+            staged = sbuf.tile([P, N // P, width], F32, name="staged%d" % piece)
             for u in range(N // P):
-                acc = psum.tile([P, width], F32, name="grad", bufs=5)
+                acc = psum.tile([P, width], F32, name="total", bufs=SUM_BANKS)
                 for c0 in range(0, width, step):
                     for a in range(PASSES):
                         nc.tensor.matmul_mx(
                             out=acc[:, c0 : c0 + step],
                             lhsT=w4_codes[:, a, 2 * P * u : 2 * P * (u + 1)].bitcast(FP4X4),
-                            lhsT_scale=w4_plane[:, a, P * u : P * (u + 1)],
+                            lhsT_scale=w4_scale_tile[:, a, P * u : P * (u + 1)],
                             rhs=h_codes[:, a, j0 + c0 : j0 + c0 + step].bitcast(FP8X4),
                             rhs_scale=h_scales[:, a, j0 + c0 : j0 + c0 + step],
                             start=(a == 0),
                             stop=(a == PASSES - 1),
                         )
-                if engines[u] == "s":
-                    nc.scalar.copy(staged[:, u, :], acc[:])
-                else:
+                if u == 0 and first_engine == "vector":
                     nc.vector.tensor_copy(staged[:, u, :], acc[:])
-            nc.sync.dma_start(out_v[:, :, j0:j1], staged[:])
+                else:
+                    nc.scalar.copy(staged[:, u, :], acc[:])
+            nc.sync.dma_start(out_rows[:, :, j0:j1], staged[:])
 
-        round_w("x", 0, 0, 512, "scalar")
-        gather_scales(0, 512)
-        gather_scales(512, 1024)
-        quantize_w("x", 0, 0, 512)
-        gather_words(0, 512)
-        gradient("x", 0)
-        gradient("x", 2)
-        round_w("y", 0, 0, 512)
-        gradient("x", 4)
-        gradient("x", 6)
-        gather_words(512, 1024)
-        quantize_w("y", 0, 0, 512)
-        gradient("x", 1)
-        gradient("y", 0)
-        round_w("x", 1, 0, 512)
-        gradient("y", 1)
-        round_w("y", 1, 0, 512)
-        gradient("y", 2)
-        length(0)
-        length(1)
-        quantize_w("x", 1, 0, 512)
-        quantize_w("y", 1, 0, 512)
-        gradient("x", 3)
-        gradient("y", 3)
-        length(2)
-        flux(0, 0)
-        gradient("y", 4)
-        length(3)
-        flux(1, 0)
-        gradient("x", 5)
-        gradient("y", 5)
-        length(4)
-        flux(2, 0)
-        gradient("y", 6)
-        length(5)
-        flux(3, 0)
-        gradient("x", 7)
-        gradient("y", 7)
-        length(6)
-        flux(4, 0)
-        gradient("x", 8)
-        gradient("y", 8)
-        length(7)
-        flux(5, 0)
-        flux(6, 0)
-        gradient("x", 9)
-        gradient("y", 9)
-        length(8)
-        round_h("vector", 0, 0)
-        flux(7, 0)
-        quantize_h(0, 0)
-        round_h("vector", 0, 1)
-        gradient("x", 10)
-        gradient("y", 10)
-        length(9)
-        flux(8, 0)
-        quantize_h(0, 1)
-        flux(8, 1)
-        gradient("x", 11)
-        gradient("y", 11)
-        length(10)
-        flux(9, 0)
-        flux(9, 1)
-        gradient("x", 12)
-        gradient("y", 12)
-        length(11)
-        flux(10, 0)
-        flux(10, 1)
-        gradient("x", 13)
-        gradient("y", 13)
-        length(12)
-        flux(11, 0)
-        round_h("vector", 1, 0)
-        flux(11, 1)
-        quantize_h(1, 0)
-        gradient("x", 14)
-        gradient("y", 14)
-        length(13)
-        gradient("x", 15)
-        gradient("y", 15)
-        length(14)
-        length(15)
-        flux(12, 0)
-        flux(12, 1)
-        round_h("scalar", 1, 1)
-        flux(13, 0)
-        flux(13, 1)
+        round_w("scalar", "x", 0)
+        gather_scales(0, S // 2)
+        gather_scales(S // 2, S)
+        quantize_w("x", 0)
+        gather_words(0, S // 2)
+        gather_words(S // 2, 3 * S // 4)
+        round_w("vector", "y", 0)
+        gather_words(3 * S // 4, S)
+        quantize_w("y", 0)
+        for name in weights:
+            round_w("vector", name, 1)
+        for name in weights:
+            quantize_w(name, 1)
+        for u in EARLY_DX:
+            square("x", u)
+
+        after_flux = {
+            6: [lambda: round_h("vector", 0, 0)],
+            7: [lambda: quantize_h(0, 0), lambda: round_h("vector", 0, 1)],
+            8: [lambda: quantize_h(0, 1)],
+        }
+        last = len(UNITS) - 1
+        for u in range(last):
+            if u not in EARLY_DX:
+                square("x", u)
+            square("y", u)
+            if 1 <= u < last - 1:
+                root(u - 1)
+                flux(u - 1)
+                for job in after_flux.get(u - 1, []):
+                    job()
+
+        square("x", last)
+        square("y", last)
+        root(last - 2)
+        round_h("scalar", 1, 0)
+        root(last - 1)
+        root(last)
+        flux(last - 2)
+        round_h("vector", 1, 1)
         quantize_h(1, 1)
+        quantize_h(1, 0)
+        project(1, "scalar")
+        flux(last - 1)
         round_h("scalar", 1, 2)
-        flux(14, 0)
-        flux(14, 1)
-        flux(14, 2)
-        flux(14, 3)
-        project(0, 512, "ss")
-        flux(15, 0)
+        project(0, "scalar")
+        flux(last)
         quantize_h(1, 2)
+        project(2, "scalar")
         round_h("vector", 1, 3)
-        flux(15, 1)
-        flux(15, 2)
         quantize_h(1, 3)
-        flux(15, 3)
-        project(512, 768, "ss")
-        round_h("vector", 1, 4)
-        project(768, 896, "ss")
-        quantize_h(1, 4)
-        project(896, 1024, "vs")
+        project(3, "vector")

@@ -30,16 +30,17 @@ PIECES = (((0, 512), (512, 1024)), ((0, 512), (512, 768), (768, 896), (896, 1024
 
 UNITS = (
     [(0, t, 1, j0) for t in range(PACK) for j0, j1 in PIECES[0]]
-    + [(1, t, 1, 0) for t in range(PACK)]
-    + [(1, 0, 2, 512), (1, 2, 2, 512), (1, 0, 4, 768), (1, 0, 4, 896)]
+    + [(1, t, 1, 0) for t in range(PACK - 1)]
+    + [(1, 0, 2, 512), (1, 3, 1, 0), (1, 2, 2, 512), (1, 0, 4, 768), (1, 0, 4, 896)]
 )
-EARLY_DX = (0, 2, 4, 6, 1)
+HALF = BANK // 2
 
 GRAD_BANKS, SUM_BANKS = 4, 4
-DX_BUFS = len(EARLY_DX) + 1
-DY_BUFS = 3
+DX_BUFS = 4
+DY_BUFS = 4
 ROOT_BUFS = 8
-H_BF16_BUFS = 4
+H_BF16_BUFS = 1
+GATES = (("y", 8), ("y", 14), ("y", 15), ("x", 15))
 
 
 def tile_list_active_cell_flux_kernel(tc, tab_words, tab_scales, offs, wx, wy, gT, w4_words, w4_scales, out):
@@ -69,25 +70,38 @@ def tile_list_active_cell_flux_kernel(tc, tab_words, tab_scales, offs, wx, wy, g
         w_raw, g_rows = {}, {}
 
         def load_w(name, a):
-            w_raw[name, a] = sbuf.tile([P, PACK, BANK], F32, name="raw_%s%d" % (name, a))
+            w_raw[name, a] = sbuf.tile([P, PACK, BANK], F32, name="raw_%s%d" % (name, a), align_bytes=64)
             nc.sync.dma_start(
                 w_raw[name, a][:], weights[name][:, a * BANK : (a + 1) * BANK].rearrange("(p i) c -> p i c", i=PACK)
             )
 
-        load_w("x", 0)
+        x0_raw = {}
+
+        def load_x0(half):
+            x0_raw[half] = sbuf.tile([P, PACK, HALF], F32, name="half_raw", bufs=2)
+            nc.sync.dma_start(
+                x0_raw[half][:], wx[:, half * HALF : (half + 1) * HALF].rearrange("(p i) c -> p i c", i=PACK)
+            )
+
+        def load_g(a, t):
+            g_rows[a, t] = sbuf.tile([P, T], F32, name="g%d%d" % (a, t))
+            nc.sync.dma_start(
+                g_rows[a, t][:], gT[a * BANK : (a + 1) * BANK, :].rearrange("(p t) c -> t p c", t=PACK)[t]
+            )
+
+        load_x0(0)
         scale_rows = tab_scales[0].bitcast(I32).rearrange("(q r) c -> r q c", r=SCALE_ROWS)
         for r in range(SCALE_ROWS):
             nc.sync.dma_start(table_scales[r:P:QUAD, :], scale_rows[r])
+        load_x0(1)
         nc.sync.dma_start(table_words[:], tab_words[0].rearrange("p t i -> p (t i)").bitcast(I32))
         load_w("y", 0)
         load_w("x", 1)
         load_w("y", 1)
-        for a in range(PASSES):
-            for t in range(PACK):
-                g_rows[a, t] = sbuf.tile([P, T], F32, name="g%d%d" % (a, t))
-                nc.sync.dma_start(
-                    g_rows[a, t][:], gT[a * BANK : (a + 1) * BANK, :].rearrange("(p t) c -> t p c", t=PACK)[t]
-                )
+        for t in range(PACK):
+            load_g(0, t)
+        for t in range(PACK):
+            load_g(1, t)
         nc.sync.dma_start(w4_codes[:].bitcast(I32), w4_words.rearrange("a p b -> p a b").bitcast(I32))
         for q in range(P // QUAD):
             nc.sync.dma_start(
@@ -111,13 +125,13 @@ def tile_list_active_cell_flux_kernel(tc, tab_words, tab_scales, offs, wx, wy, g
                 nc.scalar.activation(dst, src, ACT.Copy)
 
         w_bf16, w_codes, w_scales = {}, {}, {}
-        for name in weights:
-            for a in range(PASSES):
+        for name, a in (("y", 0), ("x", 1), ("y", 1)):
+            if True:
                 w_codes[name, a] = sbuf.tile([P, BANK], U32, name="codes_%s%d" % (name, a), align_bytes=64)
                 w_scales[name, a] = sbuf.tile([P, BANK], U8, name="scales_%s%d" % (name, a), align_bytes=64)
 
-        def round_w(engine, name, a):
-            w_bf16[name, a] = sbuf.tile([P, PACK * BANK], BF16, name="w_bf16", bufs=2, align_bytes=64)
+        def round_w(engine, name, a, slot):
+            w_bf16[name, a] = sbuf.tile([P, PACK * BANK], BF16, name=slot, align_bytes=64)
             round_copy(
                 engine,
                 w_bf16[name, a][:].rearrange("p (t m i) -> p m i t", t=PACK, i=PACK),
@@ -128,6 +142,49 @@ def tile_list_active_cell_flux_kernel(tc, tab_words, tab_scales, offs, wx, wy, g
             nc.vector.quantize_mx(
                 out=w_codes[name, a][:].bitcast(FP8X4), scales=w_scales[name, a][:], in_=w_bf16[name, a][:]
             )
+
+        x0_bf16, x0_codes, x0_scales, x0_squares = {}, {}, {}, {}
+
+        def round_x0(half):
+            x0_bf16[half] = sbuf.tile([P, PACK * HALF], BF16, name="x0_bf16", bufs=2, align_bytes=64)
+            round_copy(
+                "scalar",
+                x0_bf16[half][:].rearrange("p (t m i) -> p m i t", t=PACK, i=PACK),
+                x0_raw[half][:].rearrange("p i (m t) -> p m i t", t=PACK),
+            )
+
+        def quantize_x0(half):
+            x0_codes[half] = sbuf.tile([P, HALF], U32, name="x0_codes", bufs=2, align_bytes=64)
+            x0_scales[half] = sbuf.tile([P, HALF], U8, name="x0_scales", bufs=2, align_bytes=64)
+            nc.vector.quantize_mx(out=x0_codes[half][:].bitcast(FP8X4), scales=x0_scales[half][:], in_=x0_bf16[half][:])
+
+        def square_x0(half, pair):
+            grad = psum.tile([P, 2, HALF], F32, name="grad", bufs=GRAD_BANKS)
+            for b in range(2):
+                cells = slice((2 * pair + b) * P, (2 * pair + b + 1) * P)
+                nc.tensor.matmul_mx(
+                    out=grad[:, b, :],
+                    lhsT=v_words[:, cells].bitcast(FP8X4),
+                    lhsT_scale=v_scales[:, cells],
+                    rhs=x0_codes[half][:].bitcast(FP8X4),
+                    rhs_scale=x0_scales[half][:],
+                    start=True,
+                    stop=True,
+                )
+            if half == 0:
+                x0_squares[pair] = sbuf.tile([P, 2, PACK, P], F32, name="x0_squares", bufs=4)
+            nc.scalar.activation(
+                x0_squares[pair][:, :, :, half * P // 2 : (half + 1) * P // 2],
+                grad[:].rearrange("p b (t m) -> p b t m", t=PACK),
+                ACT.Square,
+            )
+
+        def square_block(name, u, t, b):
+            a, t0, planes, j0 = UNITS[u]
+            if (name, a) == ("x", 0):
+                block = j0 // P + b
+                return x0_squares[block // 2][:, block % 2, t0 + t, :]
+            return squares[name, u][:, b, t * P : (t + 1) * P]
 
         squares, roots, h_f32, h_bf16 = {}, {}, {}, {}
         h_codes = sbuf.tile([P, PASSES, S], U32, name="h_codes", align_bytes=64)
@@ -148,9 +205,12 @@ def tile_list_active_cell_flux_kernel(tc, tab_words, tab_scales, offs, wx, wy, g
                     start=True,
                     stop=True,
                 )
-            squares[name, u] = sbuf.tile(
-                [P, PACK // planes, planes * P], F32, name="square_" + name, bufs=DX_BUFS if name == "x" else DY_BUFS
-            )
+            if (name, u) in GATES:
+                squares[name, u] = sbuf.tile([P, PACK // planes, planes * P], F32, name="gate%s%d" % (name, u), align_bytes=64)
+            else:
+                squares[name, u] = sbuf.tile(
+                    [P, PACK // planes, planes * P], F32, name="square_" + name, bufs=DX_BUFS if name == "x" else DY_BUFS
+                )
             nc.scalar.activation(squares[name, u][:], grad[:], ACT.Square)
 
         def root(u):
@@ -161,7 +221,7 @@ def tile_list_active_cell_flux_kernel(tc, tab_words, tab_scales, offs, wx, wy, g
                     for name in ("y", "x"):
                         nc.tensor.matmul(
                             total[:, t, b * P : (b + 1) * P],
-                            squares[name, u][:, b, t * P : (t + 1) * P],
+                            square_block(name, u, t, b),
                             ident[:],
                             start=(name == "y"),
                             stop=(name == "x"),
@@ -175,7 +235,8 @@ def tile_list_active_cell_flux_kernel(tc, tab_words, tab_scales, offs, wx, wy, g
             width = BANK // planes
             piece = PIECES[a].index((j0, j0 + width))
             if t0 == 0:
-                h_f32[a, piece] = sbuf.tile([P, PACK, width], F32, name="h_f32_%d_%d" % (a, piece))
+                slot = {(1, 0): "raw_y0", (1, 1): "raw_x1", (1, 3): "gatey15"}.get((a, piece), "h_f32_%d_%d" % (a, piece))
+                h_f32[a, piece] = sbuf.tile([P, PACK, width], F32, name=slot, align_bytes=64)
             for t in range(planes):
                 nc.vector.tensor_tensor(
                     h_f32[a, piece][:, t0 + t, :],
@@ -184,9 +245,12 @@ def tile_list_active_cell_flux_kernel(tc, tab_words, tab_scales, offs, wx, wy, g
                     MULT,
                 )
 
-        def round_h(engine, a, piece):
+        def round_h(engine, a, piece, gate=None):
             j0, j1 = PIECES[a][piece]
-            h_bf16[a, piece] = sbuf.tile([P, PACK * (j1 - j0)], BF16, name="h_bf16", bufs=H_BF16_BUFS, align_bytes=64)
+            if gate is None:
+                h_bf16[a, piece] = sbuf.tile([P, PACK * (j1 - j0)], BF16, name="bf16", bufs=H_BF16_BUFS, align_bytes=64)
+            else:
+                h_bf16[a, piece] = sbuf.tile([P, PACK * (j1 - j0)], BF16, name=gate, align_bytes=64)
             round_copy(
                 engine,
                 h_bf16[a, piece][:].rearrange("p (c i t) -> p c t i", i=LINE, t=PACK),
@@ -199,15 +263,39 @@ def tile_list_active_cell_flux_kernel(tc, tab_words, tab_scales, offs, wx, wy, g
                 out=h_codes[:, a, j0:j1].bitcast(FP8X4), scales=h_scales[:, a, j0:j1], in_=h_bf16[a, piece][:]
             )
 
+        def middle():
+            both = sbuf.tile([P, 2 * PACK * BANK], BF16, name="gatey14", align_bytes=64)
+            for engine, a, piece, half in (("scalar", 0, 1, 0), ("vector", 1, 0, 1)):
+                round_copy(
+                    engine,
+                    both[:, half * PACK * BANK : (half + 1) * PACK * BANK].rearrange("p (c i t) -> p c t i", i=LINE, t=PACK),
+                    h_f32[a, piece][:].rearrange("p t (c i) -> p c t i", i=LINE),
+                )
+            nc.vector.quantize_mx(
+                out=h_codes[:].rearrange("p a j -> p (a j)")[:, BANK : 3 * BANK].bitcast(FP8X4),
+                scales=h_scales[:].rearrange("p a j -> p (a j)")[:, BANK : 3 * BANK],
+                in_=both[:],
+            )
+
+        accs = {}
+
+        def claim(piece, ring, banks):
+            j0, j1 = PIECES[1][piece]
+            for u in range(N // P):
+                accs[piece, u] = psum.tile([P, j1 - j0], F32, name=ring, bufs=banks)
+
         out_rows = out.rearrange("(u p) j -> p u j", p=P)
 
         def project(piece, first_engine):
             j0, j1 = PIECES[1][piece]
             width = j1 - j0
             step = BANK if width == BANK else P
-            staged = sbuf.tile([P, N // P, width], F32, name="staged%d" % piece)
+            if piece < 2:
+                staged = sbuf.tile([P, N // P, width], F32, name="half_raw", bufs=2)
+            else:
+                staged = sbuf.tile([P, N // P, width], F32, name="staged%d" % piece)
             for u in range(N // P):
-                acc = psum.tile([P, width], F32, name="total", bufs=SUM_BANKS)
+                acc = accs[piece, u]
                 for c0 in range(0, width, step):
                     for a in range(PASSES):
                         nc.tensor.matmul_mx(
@@ -225,55 +313,59 @@ def tile_list_active_cell_flux_kernel(tc, tab_words, tab_scales, offs, wx, wy, g
                     nc.scalar.copy(staged[:, u, :], acc[:])
             nc.sync.dma_start(out_rows[:, :, j0:j1], staged[:])
 
-        round_w("scalar", "x", 0)
-        gather_scales(0, S // 2)
-        gather_scales(S // 2, S)
-        quantize_w("x", 0)
-        gather_words(0, S // 2)
-        gather_words(S // 2, 3 * S // 4)
-        round_w("vector", "y", 0)
-        gather_words(3 * S // 4, S)
+        for half in range(2):
+            round_x0(half)
+        quantize_x0(0)
+        gather_scales(0, S)
+        quantize_x0(1)
+        for pair in range(4):
+            gather_words(2 * P * pair, 2 * P * (pair + 1))
+        round_w("vector", "y", 0, "slot_w")
         quantize_w("y", 0)
-        for name in weights:
-            round_w("vector", name, 1)
-        for name in weights:
-            quantize_w(name, 1)
-        for u in EARLY_DX:
-            square("x", u)
+        round_w("vector", "x", 1, "slot_w")
+        quantize_w("x", 1)
+        round_w("vector", "y", 1, "slot_y1")
+        quantize_w("y", 1)
+        for pair in range(4):
+            for half in range(2):
+                square_x0(half, pair)
 
         after_flux = {
-            6: [lambda: round_h("vector", 0, 0)],
-            7: [lambda: quantize_h(0, 0), lambda: round_h("vector", 0, 1)],
-            8: [lambda: quantize_h(0, 1)],
+            7: [lambda: round_h("vector", 0, 0, "gatey8")],
+            8: [lambda: quantize_h(0, 0)],
+            13: [middle],
         }
         last = len(UNITS) - 1
-        for u in range(last):
-            if u not in EARLY_DX:
+
+        def finish(u):
+            root(u)
+            flux(u)
+            for job in after_flux.get(u, []):
+                job()
+
+        early_dx = {3: 8, 5: 9, 7: 10}
+        for u in range(last + 1):
+            if u > 10:
                 square("x", u)
             square("y", u)
-            if 1 <= u < last - 1:
-                root(u - 1)
-                flux(u - 1)
-                for job in after_flux.get(u - 1, []):
-                    job()
-
-        square("x", last)
-        square("y", last)
-        root(last - 2)
-        round_h("scalar", 1, 0)
-        root(last - 1)
+            if u in early_dx:
+                square("x", early_dx[u])
+            if u >= 2:
+                finish(u - 2)
+        finish(last - 1)
         root(last)
-        flux(last - 2)
-        round_h("vector", 1, 1)
-        quantize_h(1, 1)
-        quantize_h(1, 0)
-        project(1, "scalar")
-        flux(last - 1)
-        round_h("scalar", 1, 2)
+        claim(3, "total", SUM_BANKS)
+        claim(0, "total", SUM_BANKS)
+        claim(1, "grad", GRAD_BANKS)
+        claim(2, "grad", GRAD_BANKS)
+        round_h("scalar", 1, 1, "gatey15")
+        round_h("scalar", 1, 2, "gatex15")
         project(0, "scalar")
+        quantize_h(1, 1)
         flux(last)
+        project(1, "scalar")
         quantize_h(1, 2)
-        project(2, "scalar")
         round_h("vector", 1, 3)
+        project(2, "scalar")
         quantize_h(1, 3)
         project(3, "vector")

@@ -33,14 +33,18 @@ UNITS = (
     + [(1, t, 1, 0) for t in range(PACK - 1)]
     + [(1, 0, 2, 512), (1, 3, 1, 0), (1, 2, 2, 512), (1, 0, 4, 768), (1, 0, 4, 896)]
 )
+LAST = len(UNITS) - 1
+PASS0_END = 7
+WIDE_END = 13
+LAG = 2
+EARLY_DX = {3: 8, 5: 9, 7: 10}
 HALF = BANK // 2
+SPLIT = 384
 
 GRAD_BANKS, SUM_BANKS = 4, 4
-DX_BUFS = 4
-DY_BUFS = 4
+SQUARE_BUFS = 4
 ROOT_BUFS = 8
-H_BF16_BUFS = 1
-GATES = (("y", 8), ("y", 14), ("y", 15), ("x", 15))
+HANDED_ON = (("y", PASS0_END + 1), ("y", LAST - 1), ("y", LAST), ("x", LAST), ("x", LAST - 1))
 
 
 def tile_list_active_cell_flux_kernel(tc, tab_words, tab_scales, offs, wx, wy, gT, w4_words, w4_scales, out):
@@ -98,10 +102,9 @@ def tile_list_active_cell_flux_kernel(tc, tab_words, tab_scales, offs, wx, wy, g
         load_w("y", 0)
         load_w("x", 1)
         load_w("y", 1)
-        for t in range(PACK):
-            load_g(0, t)
-        for t in range(PACK):
-            load_g(1, t)
+        for a in range(PASSES):
+            for t in range(PACK):
+                load_g(a, t)
         nc.sync.dma_start(w4_codes[:].bitcast(I32), w4_words.rearrange("a p b -> p a b").bitcast(I32))
         for q in range(P // QUAD):
             nc.sync.dma_start(
@@ -126,14 +129,12 @@ def tile_list_active_cell_flux_kernel(tc, tab_words, tab_scales, offs, wx, wy, g
 
         w_bf16, w_codes, w_scales = {}, {}, {}
         for name, a in (("y", 0), ("x", 1), ("y", 1)):
-            if True:
-                w_codes[name, a] = sbuf.tile([P, BANK], U32, name="codes_%s%d" % (name, a), align_bytes=64)
-                w_scales[name, a] = sbuf.tile([P, BANK], U8, name="scales_%s%d" % (name, a), align_bytes=64)
+            w_codes[name, a] = sbuf.tile([P, BANK], U32, name="codes_%s%d" % (name, a), align_bytes=64)
+            w_scales[name, a] = sbuf.tile([P, BANK], U8, name="scales_%s%d" % (name, a), align_bytes=64)
 
-        def round_w(engine, name, a, slot):
+        def round_w(name, a, slot):
             w_bf16[name, a] = sbuf.tile([P, PACK * BANK], BF16, name=slot, align_bytes=64)
-            round_copy(
-                engine,
+            nc.vector.tensor_copy(
                 w_bf16[name, a][:].rearrange("p (t m i) -> p m i t", t=PACK, i=PACK),
                 w_raw[name, a][:].rearrange("p i (m t) -> p m i t", t=PACK),
             )
@@ -147,14 +148,14 @@ def tile_list_active_cell_flux_kernel(tc, tab_words, tab_scales, offs, wx, wy, g
 
         def round_x0(half):
             x0_bf16[half] = sbuf.tile([P, PACK * HALF], BF16, name="x0_bf16", bufs=2, align_bytes=64)
-            round_copy(
-                "scalar",
+            nc.scalar.activation(
                 x0_bf16[half][:].rearrange("p (t m i) -> p m i t", t=PACK, i=PACK),
                 x0_raw[half][:].rearrange("p i (m t) -> p m i t", t=PACK),
+                ACT.Copy,
             )
 
         def quantize_x0(half):
-            x0_codes[half] = sbuf.tile([P, HALF], U32, name="x0_codes", bufs=2, align_bytes=64)
+            x0_codes[half] = sbuf.tile([P, HALF], U32, name="x0_codes%d" % half, align_bytes=64)
             x0_scales[half] = sbuf.tile([P, HALF], U8, name="x0_scales", bufs=2, align_bytes=64)
             nc.vector.quantize_mx(out=x0_codes[half][:].bitcast(FP8X4), scales=x0_scales[half][:], in_=x0_bf16[half][:])
 
@@ -186,6 +187,9 @@ def tile_list_active_cell_flux_kernel(tc, tab_words, tab_scales, offs, wx, wy, g
                 return x0_squares[block // 2][:, block % 2, t0 + t, :]
             return squares[name, u][:, b, t * P : (t + 1) * P]
 
+        def square_slot(name, u):
+            return "square_%s%d" % (name, u)
+
         squares, roots, h_f32, h_bf16 = {}, {}, {}, {}
         h_codes = sbuf.tile([P, PASSES, S], U32, name="h_codes", align_bytes=64)
         h_scales = sbuf.tile([P, PASSES, S], U8, name="h_scales", align_bytes=64)
@@ -205,12 +209,11 @@ def tile_list_active_cell_flux_kernel(tc, tab_words, tab_scales, offs, wx, wy, g
                     start=True,
                     stop=True,
                 )
-            if (name, u) in GATES:
-                squares[name, u] = sbuf.tile([P, PACK // planes, planes * P], F32, name="gate%s%d" % (name, u), align_bytes=64)
+            shape = [P, PACK // planes, planes * P]
+            if (name, u) in HANDED_ON:
+                squares[name, u] = sbuf.tile(shape, F32, name=square_slot(name, u), align_bytes=64)
             else:
-                squares[name, u] = sbuf.tile(
-                    [P, PACK // planes, planes * P], F32, name="square_" + name, bufs=DX_BUFS if name == "x" else DY_BUFS
-                )
+                squares[name, u] = sbuf.tile(shape, F32, name="square_" + name, bufs=SQUARE_BUFS)
             nc.scalar.activation(squares[name, u][:], grad[:], ACT.Square)
 
         def root(u):
@@ -230,12 +233,14 @@ def tile_list_active_cell_flux_kernel(tc, tab_words, tab_scales, offs, wx, wy, g
             roots[u] = sbuf.tile([P, planes, BANK // planes], F32, name="root", bufs=ROOT_BUFS)
             nc.scalar.activation(roots[u][:], total[:], ACT.Sqrt)
 
+        h_f32_slots = {(1, 0): "raw_y0", (1, 1): "raw_x1", (1, 3): square_slot("y", LAST)}
+
         def flux(u):
             a, t0, planes, j0 = UNITS[u]
             width = BANK // planes
             piece = PIECES[a].index((j0, j0 + width))
             if t0 == 0:
-                slot = {(1, 0): "raw_y0", (1, 1): "raw_x1", (1, 3): "gatey15"}.get((a, piece), "h_f32_%d_%d" % (a, piece))
+                slot = h_f32_slots.get((a, piece), "h_f32_%d_%d" % (a, piece))
                 h_f32[a, piece] = sbuf.tile([P, PACK, width], F32, name=slot, align_bytes=64)
             for t in range(planes):
                 nc.vector.tensor_tensor(
@@ -245,36 +250,20 @@ def tile_list_active_cell_flux_kernel(tc, tab_words, tab_scales, offs, wx, wy, g
                     MULT,
                 )
 
-        def round_h(engine, a, piece, gate=None):
+        def round_h(a, piece, slot, shares):
             j0, j1 = PIECES[a][piece]
-            if gate is None:
-                h_bf16[a, piece] = sbuf.tile([P, PACK * (j1 - j0)], BF16, name="bf16", bufs=H_BF16_BUFS, align_bytes=64)
-            else:
-                h_bf16[a, piece] = sbuf.tile([P, PACK * (j1 - j0)], BF16, name=gate, align_bytes=64)
-            round_copy(
-                engine,
-                h_bf16[a, piece][:].rearrange("p (c i t) -> p c t i", i=LINE, t=PACK),
-                h_f32[a, piece][:].rearrange("p t (c i) -> p c t i", i=LINE),
-            )
+            h_bf16[a, piece] = sbuf.tile([P, PACK * (j1 - j0)], BF16, name=slot, align_bytes=64)
+            for engine, c0, c1 in shares:
+                round_copy(
+                    engine,
+                    h_bf16[a, piece][:, PACK * c0 : PACK * c1].rearrange("p (c i t) -> p c t i", i=LINE, t=PACK),
+                    h_f32[a, piece][:, :, c0:c1].rearrange("p t (c i) -> p c t i", i=LINE),
+                )
 
         def quantize_h(a, piece):
             j0, j1 = PIECES[a][piece]
             nc.vector.quantize_mx(
                 out=h_codes[:, a, j0:j1].bitcast(FP8X4), scales=h_scales[:, a, j0:j1], in_=h_bf16[a, piece][:]
-            )
-
-        def middle():
-            both = sbuf.tile([P, 2 * PACK * BANK], BF16, name="gatey14", align_bytes=64)
-            for engine, a, piece, half in (("scalar", 0, 1, 0), ("vector", 1, 0, 1)):
-                round_copy(
-                    engine,
-                    both[:, half * PACK * BANK : (half + 1) * PACK * BANK].rearrange("p (c i t) -> p c t i", i=LINE, t=PACK),
-                    h_f32[a, piece][:].rearrange("p t (c i) -> p c t i", i=LINE),
-                )
-            nc.vector.quantize_mx(
-                out=h_codes[:].rearrange("p a j -> p (a j)")[:, BANK : 3 * BANK].bitcast(FP8X4),
-                scales=h_scales[:].rearrange("p a j -> p (a j)")[:, BANK : 3 * BANK],
-                in_=both[:],
             )
 
         accs = {}
@@ -290,7 +279,7 @@ def tile_list_active_cell_flux_kernel(tc, tab_words, tab_scales, offs, wx, wy, g
             j0, j1 = PIECES[1][piece]
             width = j1 - j0
             step = BANK if width == BANK else P
-            if piece < 2:
+            if width >= HALF:
                 staged = sbuf.tile([P, N // P, width], F32, name="half_raw", bufs=2)
             else:
                 staged = sbuf.tile([P, N // P, width], F32, name="staged%d" % piece)
@@ -318,54 +307,54 @@ def tile_list_active_cell_flux_kernel(tc, tab_words, tab_scales, offs, wx, wy, g
         quantize_x0(0)
         gather_scales(0, S)
         quantize_x0(1)
-        for pair in range(4):
+        for pair in range(S // HALF):
             gather_words(2 * P * pair, 2 * P * (pair + 1))
-        round_w("vector", "y", 0, "slot_w")
+        round_w("y", 0, "y_bf16")
         quantize_w("y", 0)
-        round_w("vector", "x", 1, "slot_w")
-        quantize_w("x", 1)
-        round_w("vector", "y", 1, "slot_y1")
-        quantize_w("y", 1)
-        for pair in range(4):
+        for pair in range(S // HALF):
             for half in range(2):
                 square_x0(half, pair)
-
-        after_flux = {
-            7: [lambda: round_h("vector", 0, 0, "gatey8")],
-            8: [lambda: quantize_h(0, 0)],
-            13: [middle],
-        }
-        last = len(UNITS) - 1
+        round_w("x", 1, "x0_codes1")
+        quantize_w("x", 1)
+        round_w("y", 1, "y_bf16")
+        quantize_w("y", 1)
 
         def finish(u):
             root(u)
             flux(u)
-            for job in after_flux.get(u, []):
-                job()
+            if u == PASS0_END:
+                round_h(0, 0, square_slot("y", u + 1), [("vector", 0, BANK)])
+            if u == PASS0_END + 1:
+                quantize_h(0, 0)
+            if u == WIDE_END:
+                round_h(1, 0, square_slot("x", u + 1), [("scalar", SPLIT, BANK), ("vector", 0, SPLIT)])
+                round_h(0, 1, square_slot("y", u + 1), [("scalar", 0, BANK)])
+                quantize_h(1, 0)
+                quantize_h(0, 1)
 
-        early_dx = {3: 8, 5: 9, 7: 10}
-        for u in range(last + 1):
-            if u > 10:
+        for u in range(LAST + 1):
+            if UNITS[u][0] == 1 and u not in EARLY_DX.values():
                 square("x", u)
             square("y", u)
-            if u in early_dx:
-                square("x", early_dx[u])
-            if u >= 2:
-                finish(u - 2)
-        finish(last - 1)
-        root(last)
+            if u in EARLY_DX:
+                square("x", EARLY_DX[u])
+            if u >= LAG:
+                finish(u - LAG)
+        finish(LAST - 1)
+        root(LAST)
+
         claim(3, "total", SUM_BANKS)
         claim(0, "total", SUM_BANKS)
         claim(1, "grad", GRAD_BANKS)
         claim(2, "grad", GRAD_BANKS)
-        round_h("scalar", 1, 1, "gatey15")
-        round_h("scalar", 1, 2, "gatex15")
+        round_h(1, 1, square_slot("y", LAST), [("scalar", 0, HALF)])
         project(0, "scalar")
+        round_h(1, 2, square_slot("x", LAST), [("scalar", 0, P)])
         quantize_h(1, 1)
-        flux(last)
+        flux(LAST)
         project(1, "scalar")
         quantize_h(1, 2)
-        round_h("vector", 1, 3)
+        round_h(1, 3, "h_bf16_last", [("vector", 0, P)])
         project(2, "scalar")
         quantize_h(1, 3)
         project(3, "vector")

@@ -44,7 +44,7 @@ SPLIT = 384
 GRAD_BANKS, SUM_BANKS = 4, 4
 SQUARE_BUFS = 4
 ROOT_BUFS = 8
-HANDED_ON = (("y", PASS0_END + 1), ("y", LAST - 1), ("y", LAST), ("x", LAST), ("x", LAST - 1))
+HANDED_ON = (("y", PASS0_END + 2), ("y", LAST - 1), ("y", LAST), ("x", LAST), ("x", LAST - 1))
 
 
 def tile_list_active_cell_flux_kernel(tc, tab_words, tab_scales, offs, wx, wy, gT, w4_words, w4_scales, out):
@@ -323,7 +323,7 @@ def tile_list_active_cell_flux_kernel(tc, tab_words, tab_scales, offs, wx, wy, g
             root(u)
             flux(u)
             if u == PASS0_END:
-                round_h(0, 0, square_slot("y", u + 1), [("vector", 0, BANK)])
+                round_h(0, 0, square_slot("y", u + 2), [("vector", 0, BANK)])
             if u == PASS0_END + 1:
                 quantize_h(0, 0)
             if u == WIDE_END:
@@ -332,14 +332,16 @@ def tile_list_active_cell_flux_kernel(tc, tab_words, tab_scales, offs, wx, wy, g
                 quantize_h(1, 0)
                 quantize_h(0, 1)
 
-        for u in range(LAST + 1):
-            if UNITS[u][0] == 1 and u not in EARLY_DX.values():
-                square("x", u)
-            square("y", u)
-            if u in EARLY_DX:
-                square("x", EARLY_DX[u])
-            if u >= LAG:
-                finish(u - LAG)
+        for first in range(0, LAST + 1, LAG):
+            for u in range(first, first + LAG):
+                if UNITS[u][0] == 1 and u not in EARLY_DX.values():
+                    square("x", u)
+                square("y", u)
+                if u in EARLY_DX:
+                    square("x", EARLY_DX[u])
+            if first >= LAG:
+                for u in range(first - LAG, first):
+                    finish(u)
         finish(LAST - 1)
         root(LAST)
 

@@ -35,16 +35,15 @@ UNITS = (
 )
 LAST = len(UNITS) - 1
 PASS0_END = 7
-WIDE_END = 13
 LAG = 2
-EARLY_DX = {3: 8, 5: 9, 7: 10}
+EARLY_DX = {5: 8, 7: 9}
 HALF = BANK // 2
 SPLIT = 384
 
 GRAD_BANKS, SUM_BANKS = 4, 4
 SQUARE_BUFS = 4
 ROOT_BUFS = 8
-HANDED_ON = (("y", PASS0_END + 2), ("y", LAST - 1), ("y", LAST), ("x", LAST), ("x", LAST - 1))
+HANDED_ON = (("y", PASS0_END + LAG), ("y", LAST - 1), ("y", LAST), ("x", LAST), ("x", LAST - 1))
 
 
 def tile_list_active_cell_flux_kernel(tc, tab_words, tab_scales, offs, wx, wy, gT, w4_words, w4_scales, out):
@@ -323,16 +322,11 @@ def tile_list_active_cell_flux_kernel(tc, tab_words, tab_scales, offs, wx, wy, g
             root(u)
             flux(u)
             if u == PASS0_END:
-                round_h(0, 0, square_slot("y", u + 2), [("vector", 0, BANK)])
+                round_h(0, 0, square_slot("y", u + LAG), [("vector", 0, BANK)])
             if u == PASS0_END + 1:
                 quantize_h(0, 0)
-            if u == WIDE_END:
-                round_h(1, 0, square_slot("x", u + 1), [("scalar", SPLIT, BANK), ("vector", 0, SPLIT)])
-                round_h(0, 1, square_slot("y", u + 1), [("scalar", 0, BANK)])
-                quantize_h(1, 0)
-                quantize_h(0, 1)
 
-        for first in range(0, LAST + 1, LAG):
+        for first in range(0, LAST - 1, LAG):
             for u in range(first, first + LAG):
                 if UNITS[u][0] == 1 and u not in EARLY_DX.values():
                     square("x", u)
@@ -342,6 +336,14 @@ def tile_list_active_cell_flux_kernel(tc, tab_words, tab_scales, offs, wx, wy, g
             if first >= LAG:
                 for u in range(first - LAG, first):
                     finish(u)
+        for u in (LAST - 1, LAST):
+            finish(u - LAG)
+            square("x", u)
+            square("y", u)
+        round_h(1, 0, square_slot("x", LAST - 1), [("scalar", SPLIT, BANK), ("vector", 0, SPLIT)])
+        round_h(0, 1, square_slot("y", LAST - 1), [("scalar", 0, BANK)])
+        quantize_h(1, 0)
+        quantize_h(0, 1)
         finish(LAST - 1)
         root(LAST)
 

@@ -16,6 +16,7 @@ FP8X4 = mybir.dt.float8_e4m3fn_x4
 FP4X4 = mybir.dt.float4_e2m1fn_x4
 ACT = mybir.ActivationFunctionType
 MULT = mybir.AluOpType.mult
+ADD = mybir.AluOpType.add
 
 P = 128
 PACK = 4
@@ -38,7 +39,8 @@ PASS0_END = 7
 LAG = 2
 EARLY_DX = {5: 8, 7: 9}
 HALF = BANK // 2
-SPLIT = 384
+EARLY_SCALES = 768
+SPLIT = 288
 
 GRAD_BANKS, SUM_BANKS = 4, 4
 SQUARE_BUFS = 4
@@ -51,6 +53,7 @@ def tile_list_active_cell_flux_kernel(tc, tab_words, tab_scales, offs, wx, wy, g
     with ExitStack() as ctx:
         sbuf = ctx.enter_context(tc.tile_pool(name="sbuf", bufs=1))
         psum = ctx.enter_context(tc.psum_pool(name="psum", bufs=1))
+        shared = ctx.enter_context(tc.tile_pool(name="shared", bufs=1))
 
         offsets = sbuf.tile([P, S // LIST_ROWS], U16, name="offsets")
         nc.sync.dma_start(offsets[:], offs)
@@ -66,8 +69,6 @@ def tile_list_active_cell_flux_kernel(tc, tab_words, tab_scales, offs, wx, wy, g
         ident = sbuf.tile([P, P], F32, name="ident")
         make_identity(nc, ident[:])
         nc.gpsimd.memset(w4_scale_tile[:], 0)
-        warm = sbuf.tile([P, 1], F32, name="warm")
-        nc.scalar.activation(warm[:], ident[:, 0:1], ACT.Sqrt)
 
         weights = {"x": wx, "y": wy}
         w_raw, g_rows = {}, {}
@@ -81,7 +82,10 @@ def tile_list_active_cell_flux_kernel(tc, tab_words, tab_scales, offs, wx, wy, g
         x0_raw = {}
 
         def load_x0(half):
-            x0_raw[half] = sbuf.tile([P, PACK, HALF], F32, name="half_raw", bufs=2)
+            if half == 0:
+                x0_raw[half] = sbuf.tile([P, PACK, HALF], F32, name="x0_raw0", align_bytes=64)
+            else:
+                x0_raw[half] = shared.tile([P, PACK, HALF], F32, name="x0_raw1", align_bytes=64, offset=0)
             nc.sync.dma_start(
                 x0_raw[half][:], wx[:, half * HALF : (half + 1) * HALF].rearrange("(p i) c -> p i c", i=PACK)
             )
@@ -93,11 +97,13 @@ def tile_list_active_cell_flux_kernel(tc, tab_words, tab_scales, offs, wx, wy, g
             )
 
         load_x0(0)
+        warm = sbuf.tile([P, 1], F32, name="warm")
+        nc.scalar.activation(warm[:], x0_raw[0][:, 0, 0:1], ACT.Sqrt, bias=1.0, scale=0.0)
         scale_rows = tab_scales[0].bitcast(I32).rearrange("(q r) c -> r q c", r=SCALE_ROWS)
         for r in range(SCALE_ROWS):
             nc.sync.dma_start(table_scales[r:P:QUAD, :], scale_rows[r])
-        load_x0(1)
         nc.sync.dma_start(table_words[:], tab_words[0].rearrange("p t i -> p (t i)").bitcast(I32))
+        load_x0(1)
         load_w("y", 0)
         load_w("x", 1)
         load_w("y", 1)
@@ -112,10 +118,20 @@ def tile_list_active_cell_flux_kernel(tc, tab_words, tab_scales, offs, wx, wy, g
             )
 
         v_words = sbuf.tile([P, S], I32, name="v_words", align_bytes=64)
-        v_scales = sbuf.tile([P, S], U8, name="v_scales", align_bytes=64)
+        v_scales = {}
 
-        def gather_scales(j0, j1):
-            nc.vector.tensor_copy(v_scales[:, j0:j1], table_scales[:].bitcast(U8).indirect(picks(j0, j1)))
+        def gather_scales(part):
+            if part == 0:
+                j0, j1 = 0, EARLY_SCALES
+                v_scales[part] = sbuf.tile([P, j1 - j0], U8, name="v_scales0", align_bytes=64)
+            else:
+                j0, j1 = EARLY_SCALES, S
+                v_scales[part] = shared.tile([P, j1 - j0], U8, name="v_scales1", align_bytes=64, offset=0)
+            nc.vector.tensor_copy(v_scales[part][:], table_scales[:].bitcast(U8).indirect(picks(j0, j1)))
+
+        def cell_scales(cells):
+            part, c0 = divmod(cells.start, EARLY_SCALES)
+            return v_scales[part][:, c0 : c0 + P]
 
         def gather_words(j0, j1):
             nc.vector.tensor_copy(v_words[:, j0:j1].bitcast(U32), table_words[:].bitcast(U32).indirect(picks(j0, j1)))
@@ -132,50 +148,68 @@ def tile_list_active_cell_flux_kernel(tc, tab_words, tab_scales, offs, wx, wy, g
             w_scales[name, a] = sbuf.tile([P, BANK], U8, name="scales_%s%d" % (name, a), align_bytes=64)
 
         def round_w(name, a, slot):
-            w_bf16[name, a] = sbuf.tile([P, PACK * BANK], BF16, name=slot, align_bytes=64)
-            nc.vector.tensor_copy(
-                w_bf16[name, a][:].rearrange("p (t m i) -> p m i t", t=PACK, i=PACK),
-                w_raw[name, a][:].rearrange("p i (m t) -> p m i t", t=PACK),
-            )
+            if name == "y":
+                w_bf16[name, a] = shared.tile([P, PACK * BANK], BF16, name=slot, align_bytes=64, offset=256)
+            else:
+                w_bf16[name, a] = sbuf.tile([P, PACK * BANK], BF16, name=slot, align_bytes=64)
+            for t0 in (0, 2):
+                nc.vector.tensor_copy(
+                    w_bf16[name, a][:].rearrange("p (t m i) -> p m i t", t=PACK, i=PACK)[:, :, :, t0 : t0 + 2],
+                    w_raw[name, a][:].rearrange("p i (m t) -> p m i t", t=PACK)[:, :, :, t0 : t0 + 2],
+                )
 
         def quantize_w(name, a):
-            nc.vector.quantize_mx(
-                out=w_codes[name, a][:].bitcast(FP8X4), scales=w_scales[name, a][:], in_=w_bf16[name, a][:]
-            )
+            for c0 in (0, HALF):
+                nc.vector.quantize_mx(
+                    out=w_codes[name, a][:, c0 : c0 + HALF].bitcast(FP8X4),
+                    scales=w_scales[name, a][:, c0 : c0 + HALF],
+                    in_=w_bf16[name, a][:, PACK * c0 : PACK * (c0 + HALF)],
+                )
 
         x0_bf16, x0_codes, x0_scales, x0_squares = {}, {}, {}, {}
 
         def round_x0(half):
-            x0_bf16[half] = sbuf.tile([P, PACK * HALF], BF16, name="x0_bf16", bufs=2, align_bytes=64)
-            nc.scalar.activation(
-                x0_bf16[half][:].rearrange("p (t m i) -> p m i t", t=PACK, i=PACK),
-                x0_raw[half][:].rearrange("p i (m t) -> p m i t", t=PACK),
-                ACT.Copy,
-            )
+            if half == 0:
+                x0_bf16[half] = sbuf.tile([P, PACK * HALF], BF16, name="x0_bf16", align_bytes=64)
+                nc.scalar.activation(
+                    x0_bf16[half][:].rearrange("p (c l i) -> p c i l", l=LINE, i=PACK),
+                    x0_raw[half][:].rearrange("p i (c l) -> p c i l", l=LINE),
+                    ACT.Copy,
+                )
+            else:
+                x0_bf16[half] = sbuf.tile([P, PACK * HALF], BF16, name="x0_bf16_b", align_bytes=64)
+                nc.gpsimd.tensor_scalar(
+                    x0_bf16[half][:].rearrange("p (c i) -> p c i", i=PACK),
+                    x0_raw[half][:].rearrange("p i c -> p c i"),
+                    1.0,
+                    0.0,
+                    MULT,
+                    ADD,
+                )
 
         def quantize_x0(half):
             x0_codes[half] = sbuf.tile([P, HALF], U32, name="x0_codes%d" % half, align_bytes=64)
             x0_scales[half] = sbuf.tile([P, HALF], U8, name="x0_scales", bufs=2, align_bytes=64)
             nc.vector.quantize_mx(out=x0_codes[half][:].bitcast(FP8X4), scales=x0_scales[half][:], in_=x0_bf16[half][:])
 
-        def square_x0(half, pair):
-            grad = psum.tile([P, 2, HALF], F32, name="grad", bufs=GRAD_BANKS)
-            for b in range(2):
+        def square_x0(half, pair, b0, b1):
+            if half == 0 and b0 == 0:
+                x0_squares[pair] = sbuf.tile([P, 2, PACK, P], F32, name="x0_squares", bufs=4)
+            grad = psum.tile([P, b1 - b0, HALF], F32, name="grad", bufs=GRAD_BANKS)
+            for b in range(b0, b1):
                 cells = slice((2 * pair + b) * P, (2 * pair + b + 1) * P)
                 nc.tensor.matmul_mx(
-                    out=grad[:, b, :],
+                    out=grad[:, b - b0, :],
                     lhsT=v_words[:, cells].bitcast(FP8X4),
-                    lhsT_scale=v_scales[:, cells],
+                    lhsT_scale=cell_scales(cells),
                     rhs=x0_codes[half][:].bitcast(FP8X4),
                     rhs_scale=x0_scales[half][:],
                     start=True,
                     stop=True,
                 )
-            if half == 0:
-                x0_squares[pair] = sbuf.tile([P, 2, PACK, P], F32, name="x0_squares", bufs=4)
             nc.scalar.activation(
-                x0_squares[pair][:, :, :, half * P // 2 : (half + 1) * P // 2],
-                grad[:].rearrange("p b (t m) -> p b t m", t=PACK),
+                x0_squares[pair][:, b0:b1, :, half * P // 2 : (half + 1) * P // 2],
+                grad[:].rearrange("p b (m t) -> p b t m", t=PACK),
                 ACT.Square,
             )
 
@@ -202,7 +236,7 @@ def tile_list_active_cell_flux_kernel(tc, tab_words, tab_scales, offs, wx, wy, g
                 nc.tensor.matmul_mx(
                     out=grad[:, b, :],
                     lhsT=v_words[:, cells].bitcast(FP8X4),
-                    lhsT_scale=v_scales[:, cells],
+                    lhsT_scale=cell_scales(cells),
                     rhs=w_codes[name, a][:, rows].bitcast(FP8X4),
                     rhs_scale=w_scales[name, a][:, rows],
                     start=True,
@@ -279,7 +313,7 @@ def tile_list_active_cell_flux_kernel(tc, tab_words, tab_scales, offs, wx, wy, g
             width = j1 - j0
             step = BANK if width == BANK else P
             if width >= HALF:
-                staged = sbuf.tile([P, N // P, width], F32, name="half_raw", bufs=2)
+                staged = sbuf.tile([P, N // P, width], F32, name="staged_wide", bufs=2)
             else:
                 staged = sbuf.tile([P, N // P, width], F32, name="staged%d" % piece)
             for u in range(N // P):
@@ -301,18 +335,24 @@ def tile_list_active_cell_flux_kernel(tc, tab_words, tab_scales, offs, wx, wy, g
                     nc.scalar.copy(staged[:, u, :], acc[:])
             nc.sync.dma_start(out_rows[:, :, j0:j1], staged[:])
 
-        for half in range(2):
-            round_x0(half)
+        gather_scales(0)
+        round_x0(0)
         quantize_x0(0)
-        gather_scales(0, S)
-        quantize_x0(1)
         for pair in range(S // HALF):
             gather_words(2 * P * pair, 2 * P * (pair + 1))
+        round_x0(1)
+        quantize_x0(1)
+        gather_scales(1)
         round_w("y", 0, "y_bf16")
         quantize_w("y", 0)
-        for pair in range(S // HALF):
+        for pairs in (range(3), range(3, 4)):
             for half in range(2):
-                square_x0(half, pair)
+                for pair in pairs:
+                    if half == 0 and pair == 0:
+                        square_x0(half, pair, 0, 1)
+                        square_x0(half, pair, 1, 2)
+                    else:
+                        square_x0(half, pair, 0, 2)
         round_w("x", 1, "x0_codes1")
         quantize_w("x", 1)
         round_w("y", 1, "y_bf16")

@@ -16,7 +16,6 @@ FP8X4 = mybir.dt.float8_e4m3fn_x4
 FP4X4 = mybir.dt.float4_e2m1fn_x4
 ACT = mybir.ActivationFunctionType
 MULT = mybir.AluOpType.mult
-ADD = mybir.AluOpType.add
 
 P = 128
 PACK = 4
@@ -40,7 +39,7 @@ LAG = 2
 EARLY_DX = {5: 8, 7: 9}
 HALF = BANK // 2
 EARLY_SCALES = 768
-SPLIT = 288
+SPLIT = 320
 
 GRAD_BANKS, SUM_BANKS = 4, 4
 SQUARE_BUFS = 4
@@ -85,7 +84,7 @@ def tile_list_active_cell_flux_kernel(tc, tab_words, tab_scales, offs, wx, wy, g
             if half == 0:
                 x0_raw[half] = sbuf.tile([P, PACK, HALF], F32, name="x0_raw0", align_bytes=64)
             else:
-                x0_raw[half] = shared.tile([P, PACK, HALF], F32, name="x0_raw1", align_bytes=64, offset=0)
+                x0_raw[half] = shared.tile([P, PACK, HALF], F32, name="x0_raw1", align_bytes=64, offset=16128)
             nc.sync.dma_start(
                 x0_raw[half][:], wx[:, half * HALF : (half + 1) * HALF].rearrange("(p i) c -> p i c", i=PACK)
             )
@@ -126,7 +125,7 @@ def tile_list_active_cell_flux_kernel(tc, tab_words, tab_scales, offs, wx, wy, g
                 v_scales[part] = sbuf.tile([P, j1 - j0], U8, name="v_scales0", align_bytes=64)
             else:
                 j0, j1 = EARLY_SCALES, S
-                v_scales[part] = shared.tile([P, j1 - j0], U8, name="v_scales1", align_bytes=64, offset=0)
+                v_scales[part] = shared.tile([P, j1 - j0], U8, name="v_scales1", align_bytes=64, offset=16384)
             nc.vector.tensor_copy(v_scales[part][:], table_scales[:].bitcast(U8).indirect(picks(j0, j1)))
 
         def cell_scales(cells):
@@ -149,7 +148,7 @@ def tile_list_active_cell_flux_kernel(tc, tab_words, tab_scales, offs, wx, wy, g
 
         def round_w(name, a, slot):
             if name == "y":
-                w_bf16[name, a] = shared.tile([P, PACK * BANK], BF16, name=slot, align_bytes=64, offset=256)
+                w_bf16[name, a] = shared.tile([P, PACK * BANK], BF16, name=slot, align_bytes=64, offset=16640)
             else:
                 w_bf16[name, a] = sbuf.tile([P, PACK * BANK], BF16, name=slot, align_bytes=64)
             for t0 in (0, 2):
@@ -166,26 +165,16 @@ def tile_list_active_cell_flux_kernel(tc, tab_words, tab_scales, offs, wx, wy, g
                     in_=w_bf16[name, a][:, PACK * c0 : PACK * (c0 + HALF)],
                 )
 
-        x0_bf16, x0_codes, x0_scales, x0_squares = {}, {}, {}, {}
+        x0_bf16, x0_codes, x0_scales = {}, {}, {}
+        x0_squares = shared.tile([P, S // P, PACK, P], F32, name="x0_squares", align_bytes=64, offset=0)
 
         def round_x0(half):
-            if half == 0:
-                x0_bf16[half] = sbuf.tile([P, PACK * HALF], BF16, name="x0_bf16", align_bytes=64)
-                nc.scalar.activation(
-                    x0_bf16[half][:].rearrange("p (c l i) -> p c i l", l=LINE, i=PACK),
-                    x0_raw[half][:].rearrange("p i (c l) -> p c i l", l=LINE),
-                    ACT.Copy,
-                )
-            else:
-                x0_bf16[half] = sbuf.tile([P, PACK * HALF], BF16, name="x0_bf16_b", align_bytes=64)
-                nc.gpsimd.tensor_scalar(
-                    x0_bf16[half][:].rearrange("p (c i) -> p c i", i=PACK),
-                    x0_raw[half][:].rearrange("p i c -> p c i"),
-                    1.0,
-                    0.0,
-                    MULT,
-                    ADD,
-                )
+            x0_bf16[half] = sbuf.tile([P, PACK * HALF], BF16, name="x0_bf16", bufs=2, align_bytes=64)
+            nc.scalar.activation(
+                x0_bf16[half][:].rearrange("p (t m i) -> p m i t", t=PACK, i=PACK),
+                x0_raw[half][:].rearrange("p i (m t) -> p m i t", t=PACK),
+                ACT.Copy,
+            )
 
         def quantize_x0(half):
             x0_codes[half] = sbuf.tile([P, HALF], U32, name="x0_codes%d" % half, align_bytes=64)
@@ -193,8 +182,6 @@ def tile_list_active_cell_flux_kernel(tc, tab_words, tab_scales, offs, wx, wy, g
             nc.vector.quantize_mx(out=x0_codes[half][:].bitcast(FP8X4), scales=x0_scales[half][:], in_=x0_bf16[half][:])
 
         def square_x0(half, pair, b0, b1):
-            if half == 0 and b0 == 0:
-                x0_squares[pair] = sbuf.tile([P, 2, PACK, P], F32, name="x0_squares", bufs=4)
             grad = psum.tile([P, b1 - b0, HALF], F32, name="grad", bufs=GRAD_BANKS)
             for b in range(b0, b1):
                 cells = slice((2 * pair + b) * P, (2 * pair + b + 1) * P)
@@ -208,8 +195,8 @@ def tile_list_active_cell_flux_kernel(tc, tab_words, tab_scales, offs, wx, wy, g
                     stop=True,
                 )
             nc.scalar.activation(
-                x0_squares[pair][:, b0:b1, :, half * P // 2 : (half + 1) * P // 2],
-                grad[:].rearrange("p b (m t) -> p b t m", t=PACK),
+                x0_squares[:, 2 * pair + b0 : 2 * pair + b1, :, half * P // 2 : (half + 1) * P // 2],
+                grad[:].rearrange("p b (t m) -> p b t m", t=PACK),
                 ACT.Square,
             )
 
@@ -217,7 +204,7 @@ def tile_list_active_cell_flux_kernel(tc, tab_words, tab_scales, offs, wx, wy, g
             a, t0, planes, j0 = UNITS[u]
             if (name, a) == ("x", 0):
                 block = j0 // P + b
-                return x0_squares[block // 2][:, block % 2, t0 + t, :]
+                return x0_squares[:, block, t0 + t, :]
             return squares[name, u][:, b, t * P : (t + 1) * P]
 
         def square_slot(name, u):
@@ -348,11 +335,7 @@ def tile_list_active_cell_flux_kernel(tc, tab_words, tab_scales, offs, wx, wy, g
         for pairs in (range(3), range(3, 4)):
             for half in range(2):
                 for pair in pairs:
-                    if half == 0 and pair == 0:
-                        square_x0(half, pair, 0, 1)
-                        square_x0(half, pair, 1, 2)
-                    else:
-                        square_x0(half, pair, 0, 2)
+                    square_x0(half, pair, 0, 2)
         round_w("x", 1, "x0_codes1")
         quantize_w("x", 1)
         round_w("y", 1, "y_bf16")

@@ -36,7 +36,7 @@ UNITS = (
 LAST = len(UNITS) - 1
 PASS0_END = 7
 LAG = 2
-EARLY_DX = {5: 8, 7: 9}
+EARLY_DX = {3: 8, 5: 9, 7: 10, 9: 11, 11: 12}
 HALF = BANK // 2
 EARLY_SCALES = 768
 SPLIT = 320
@@ -354,11 +354,11 @@ def tile_list_active_cell_flux_kernel(tc, tab_words, tab_scales, offs, wx, wy, g
                 if UNITS[u][0] == 1 and u not in EARLY_DX.values():
                     square("x", u)
                 square("y", u)
-                if u in EARLY_DX:
-                    square("x", EARLY_DX[u])
             if first >= LAG:
                 for u in range(first - LAG, first):
                     finish(u)
+            if first + 1 in EARLY_DX:
+                square("x", EARLY_DX[first + 1])
         for u in (LAST - 1, LAST):
             finish(u - LAG)
             square("x", u)
@@ -382,6 +382,6 @@ def tile_list_active_cell_flux_kernel(tc, tab_words, tab_scales, offs, wx, wy, g
         project(1, "scalar")
         quantize_h(1, 2)
         round_h(1, 3, "h_bf16_last", [("vector", 0, P)])
-        project(2, "scalar")
+        project(2, "vector")
         quantize_h(1, 3)
         project(3, "vector")

@@ -42,6 +42,7 @@ EARLY_SCALES = 768
 SPLIT = 320
 
 GRAD_BANKS, SUM_BANKS = 4, 4
+AHEAD = (0, 2)
 SQUARE_BUFS = 4
 ROOT_BUFS = 8
 HANDED_ON = (("y", PASS0_END + LAG), ("y", LAST - 1), ("y", LAST), ("x", LAST), ("x", LAST - 1))
@@ -236,20 +237,29 @@ def tile_list_active_cell_flux_kernel(tc, tab_words, tab_scales, offs, wx, wy, g
                 squares[name, u] = sbuf.tile(shape, F32, name="square_" + name, bufs=SQUARE_BUFS)
             nc.scalar.activation(squares[name, u][:], grad[:], ACT.Square)
 
+        def turn(dst, block, start, stop):
+            nc.tensor.matmul(dst, block, ident[:], start=start, stop=stop, is_transpose=True)
+
+        totals = {}
+
+        def turn_x_ahead(u):
+            totals[u] = psum.tile([P, 1, BANK], F32, name="total_ahead", bufs=SUM_BANKS // 2)
+            for b in range(PACK):
+                turn(totals[u][:, 0, b * P : (b + 1) * P], square_block("x", u, 0, b), b == 0, False)
+
         def root(u):
             a, t0, planes, j0 = UNITS[u]
-            total = psum.tile([P, planes, BANK // planes], F32, name="total", bufs=SUM_BANKS)
-            for t in range(planes):
-                for b in range(PACK // planes):
-                    for name in ("y", "x"):
-                        nc.tensor.matmul(
-                            total[:, t, b * P : (b + 1) * P],
-                            square_block(name, u, t, b),
-                            ident[:],
-                            start=(name == "y"),
-                            stop=(name == "x"),
-                            is_transpose=True,
-                        )
+            if u in AHEAD:
+                total = totals[u]
+                for b in range(PACK):
+                    turn(total[:, 0, b * P : (b + 1) * P], square_block("y", u, 0, b), False, b == PACK - 1)
+            else:
+                name = "total_ahead" if u % 2 == 0 else "total"
+                total = psum.tile([P, planes, BANK // planes], F32, name=name, bufs=SUM_BANKS // 2)
+                for t in range(planes):
+                    for b in range(PACK // planes):
+                        for name in ("y", "x"):
+                            turn(total[:, t, b * P : (b + 1) * P], square_block(name, u, t, b), name == "y", name == "x")
             roots[u] = sbuf.tile([P, planes, BANK // planes], F32, name="root", bufs=ROOT_BUFS)
             nc.scalar.activation(roots[u][:], total[:], ACT.Sqrt)
 
@@ -288,10 +298,10 @@ def tile_list_active_cell_flux_kernel(tc, tab_words, tab_scales, offs, wx, wy, g
 
         accs = {}
 
-        def claim(piece, ring, banks):
+        def claim(piece, rings, banks):
             j0, j1 = PIECES[1][piece]
             for u in range(N // P):
-                accs[piece, u] = psum.tile([P, j1 - j0], F32, name=ring, bufs=banks)
+                accs[piece, u] = psum.tile([P, j1 - j0], F32, name=rings[u], bufs=banks)
 
         out_rows = out.rearrange("(u p) j -> p u j", p=P)
 
@@ -354,6 +364,9 @@ def tile_list_active_cell_flux_kernel(tc, tab_words, tab_scales, offs, wx, wy, g
                 if UNITS[u][0] == 1 and u not in EARLY_DX.values():
                     square("x", u)
                 square("y", u)
+            if first == 0:
+                for u in AHEAD:
+                    turn_x_ahead(u)
             if first >= LAG:
                 for u in range(first - LAG, first):
                     finish(u)
@@ -370,10 +383,10 @@ def tile_list_active_cell_flux_kernel(tc, tab_words, tab_scales, offs, wx, wy, g
         finish(LAST - 1)
         root(LAST)
 
-        claim(3, "total", SUM_BANKS)
-        claim(0, "total", SUM_BANKS)
-        claim(1, "grad", GRAD_BANKS)
-        claim(2, "grad", GRAD_BANKS)
+        claim(3, ("total_ahead", "total"), SUM_BANKS // 2)
+        claim(0, ("total_ahead", "total"), SUM_BANKS // 2)
+        claim(1, ("grad", "grad"), GRAD_BANKS)
+        claim(2, ("grad", "grad"), GRAD_BANKS)
         round_h(1, 1, square_slot("y", LAST), [("scalar", 0, HALF)])
         project(0, "scalar")
         round_h(1, 2, square_slot("x", LAST), [("scalar", 0, P)])

from contextlib import ExitStack

import concourse.mybir as mybir
from concourse.masks import make_identity

K, H, N, T, S = 512, 1024, 256, 2048, 1024
FLOPS = 2 * (2 * K * H * S + H * N * S)

F32 = mybir.dt.float32
BF16 = mybir.dt.bfloat16
I32 = mybir.dt.int32
U32 = mybir.dt.uint32
U16 = mybir.dt.uint16
U8 = mybir.dt.uint8
FP8X4 = mybir.dt.float8_e4m3fn_x4
FP4X4 = mybir.dt.float4_e2m1fn_x4
ACT = mybir.ActivationFunctionType
MULT = mybir.AluOpType.mult

P = 128
PACK = 4
BANK = P * PACK
PASSES = H // BANK
LIST_ROWS = 16
QUAD = 32
SCALE_ROWS = 4
LINE = 4

PIECES = (((0, 512), (512, 1024)), ((0, 512), (512, 768), (768, 896), (896, 1024)))

UNITS = (
    [(0, t, 1, j0) for t in range(PACK) for j0, j1 in PIECES[0]]
    + [(1, t, 1, 0) for t in range(PACK - 1)]
    + [(1, 0, 2, 512), (1, 3, 1, 0), (1, 2, 2, 512), (1, 0, 4, 768), (1, 0, 4, 896)]
)
LAST = len(UNITS) - 1
PASS0_END = 7
LAG = 2
EARLY_DX = {3: 8, 5: 9, 7: 10, 9: 11, 11: 12}
HALF = BANK // 2
EARLY_SCALES = 768
SPLIT = 320

GRAD_BANKS, SUM_BANKS = 4, 4
AHEAD = (0, 2)
SQUARE_BUFS = 4
ROOT_BUFS = 8
HANDED_ON = (("y", PASS0_END + LAG), ("y", LAST - 1), ("y", LAST), ("x", LAST), ("x", LAST - 1))


def tile_list_active_cell_flux_kernel(tc, tab_words, tab_scales, offs, wx, wy, gT, w4_words, w4_scales, out):
    nc = tc.nc
    with ExitStack() as ctx:
        sbuf = ctx.enter_context(tc.tile_pool(name="sbuf", bufs=1))
        psum = ctx.enter_context(tc.psum_pool(name="psum", bufs=1))
        shared = ctx.enter_context(tc.tile_pool(name="shared", bufs=1))

        offsets = sbuf.tile([P, S // LIST_ROWS], U16, name="offsets")
        nc.sync.dma_start(offsets[:], offs)

        def picks(j0, j1):
            return offsets[:, j0 // LIST_ROWS : j1 // LIST_ROWS]

        table_scales = sbuf.tile([P, T // 4], I32, name="table_scales", align_bytes=64)
        nc.gpsimd.memset(table_scales[:], 0)
        table_words = sbuf.tile([P, T], I32, name="table_words", align_bytes=64)
        w4_codes = sbuf.tile([P, PASSES, 2 * N], U8, name="w4_codes", align_bytes=64)
        w4_scale_tile = sbuf.tile([P, PASSES, N], U8, name="w4_scale_tile", align_bytes=64)
        ident = sbuf.tile([P, P], F32, name="ident")
        make_identity(nc, ident[:])
        nc.gpsimd.memset(w4_scale_tile[:], 0)

        weights = {"x": wx, "y": wy}
        w_raw, g_rows = {}, {}

        def load_w(name, a):
            w_raw[name, a] = sbuf.tile([P, PACK, BANK], F32, name="raw_%s%d" % (name, a), align_bytes=64)
            nc.sync.dma_start(
                w_raw[name, a][:], weights[name][:, a * BANK : (a + 1) * BANK].rearrange("(p i) c -> p i c", i=PACK)
            )

        x0_raw = {}

        def load_x0(half):
            if half == 0:
                x0_raw[half] = sbuf.tile([P, PACK, HALF], F32, name="x0_raw0", align_bytes=64)
            else:
                x0_raw[half] = shared.tile([P, PACK, HALF], F32, name="x0_raw1", align_bytes=64, offset=16128)
            nc.sync.dma_start(
                x0_raw[half][:], wx[:, half * HALF : (half + 1) * HALF].rearrange("(p i) c -> p i c", i=PACK)
            )

        def load_g(a, t):
            g_rows[a, t] = sbuf.tile([P, T], F32, name="g%d%d" % (a, t))
            nc.sync.dma_start(
                g_rows[a, t][:], gT[a * BANK : (a + 1) * BANK, :].rearrange("(p t) c -> t p c", t=PACK)[t]
            )

        load_x0(0)
        warm = sbuf.tile([P, 1], F32, name="warm")
        nc.scalar.activation(warm[:], x0_raw[0][:, 0, 0:1], ACT.Sqrt, bias=1.0, scale=0.0)
        scale_rows = tab_scales[0].bitcast(I32).rearrange("(q r) c -> r q c", r=SCALE_ROWS)
        for r in range(SCALE_ROWS):
            nc.sync.dma_start(table_scales[r:P:QUAD, :], scale_rows[r])
        nc.sync.dma_start(table_words[:], tab_words[0].rearrange("p t i -> p (t i)").bitcast(I32))
        load_x0(1)
        load_w("y", 0)
        load_w("x", 1)
        load_w("y", 1)
        for a in range(PASSES):
            for t in range(PACK):
                load_g(a, t)
        nc.sync.dma_start(w4_codes[:].bitcast(I32), w4_words.rearrange("a p b -> p a b").bitcast(I32))
        for q in range(P // QUAD):
            nc.sync.dma_start(
                w4_scale_tile[QUAD * q : QUAD * q + SCALE_ROWS].bitcast(I32),
                w4_scales[:, SCALE_ROWS * q : SCALE_ROWS * (q + 1), :].rearrange("a r n -> r a n").bitcast(I32),
            )

        v_words = sbuf.tile([P, S], I32, name="v_words", align_bytes=64)
        v_scales = {}

        def gather_scales(part):
            if part == 0:
                j0, j1 = 0, EARLY_SCALES
                v_scales[part] = sbuf.tile([P, j1 - j0], U8, name="v_scales0", align_bytes=64)
            else:
                j0, j1 = EARLY_SCALES, S
                v_scales[part] = shared.tile([P, j1 - j0], U8, name="v_scales1", align_bytes=64, offset=16384)
            nc.vector.tensor_copy(v_scales[part][:], table_scales[:].bitcast(U8).indirect(picks(j0, j1)))

        def cell_scales(cells):
            part, c0 = divmod(cells.start, EARLY_SCALES)
            return v_scales[part][:, c0 : c0 + P]

        def gather_words(j0, j1):
            nc.vector.tensor_copy(v_words[:, j0:j1].bitcast(U32), table_words[:].bitcast(U32).indirect(picks(j0, j1)))

        def round_copy(engine, dst, src):
            if engine == "vector":
                nc.vector.tensor_copy(dst, src)
            else:
                nc.scalar.activation(dst, src, ACT.Copy)

        w_bf16, w_codes, w_scales = {}, {}, {}
        for name, a in (("y", 0), ("x", 1), ("y", 1)):
            w_codes[name, a] = sbuf.tile([P, BANK], U32, name="codes_%s%d" % (name, a), align_bytes=64)
            w_scales[name, a] = sbuf.tile([P, BANK], U8, name="scales_%s%d" % (name, a), align_bytes=64)

        def round_w(name, a, slot):
            if name == "y":
                w_bf16[name, a] = shared.tile([P, PACK * BANK], BF16, name=slot, align_bytes=64, offset=16640)
            else:
                w_bf16[name, a] = sbuf.tile([P, PACK * BANK], BF16, name=slot, align_bytes=64)
            for t0 in (0, 2):
                nc.vector.tensor_copy(
                    w_bf16[name, a][:].rearrange("p (t m i) -> p m i t", t=PACK, i=PACK)[:, :, :, t0 : t0 + 2],
                    w_raw[name, a][:].rearrange("p i (m t) -> p m i t", t=PACK)[:, :, :, t0 : t0 + 2],
                )

        def quantize_w(name, a):
            for c0 in (0, HALF):
                nc.vector.quantize_mx(
                    out=w_codes[name, a][:, c0 : c0 + HALF].bitcast(FP8X4),
                    scales=w_scales[name, a][:, c0 : c0 + HALF],
                    in_=w_bf16[name, a][:, PACK * c0 : PACK * (c0 + HALF)],
                )

        x0_bf16, x0_codes, x0_scales = {}, {}, {}
        x0_squares = shared.tile([P, S // P, PACK, P], F32, name="x0_squares", align_bytes=64, offset=0)

        def round_x0(half):
            x0_bf16[half] = sbuf.tile([P, PACK * HALF], BF16, name="x0_bf16", bufs=2, align_bytes=64)
            nc.scalar.activation(
                x0_bf16[half][:].rearrange("p (t m i) -> p m i t", t=PACK, i=PACK),
                x0_raw[half][:].rearrange("p i (m t) -> p m i t", t=PACK),
                ACT.Copy,
            )

        def quantize_x0(half):
            x0_codes[half] = sbuf.tile([P, HALF], U32, name="x0_codes%d" % half, align_bytes=64)
            x0_scales[half] = sbuf.tile([P, HALF], U8, name="x0_scales", bufs=2, align_bytes=64)
            nc.vector.quantize_mx(out=x0_codes[half][:].bitcast(FP8X4), scales=x0_scales[half][:], in_=x0_bf16[half][:])

        def square_x0(half, pair, b0, b1):
            grad = psum.tile([P, b1 - b0, HALF], F32, name="grad", bufs=GRAD_BANKS)
            for b in range(b0, b1):
                cells = slice((2 * pair + b) * P, (2 * pair + b + 1) * P)
                nc.tensor.matmul_mx(
                    out=grad[:, b - b0, :],
                    lhsT=v_words[:, cells].bitcast(FP8X4),
                    lhsT_scale=cell_scales(cells),
                    rhs=x0_codes[half][:].bitcast(FP8X4),
                    rhs_scale=x0_scales[half][:],
                    start=True,
                    stop=True,
                )
            nc.scalar.activation(
                x0_squares[:, 2 * pair + b0 : 2 * pair + b1, :, half * P // 2 : (half + 1) * P // 2],
                grad[:].rearrange("p b (t m) -> p b t m", t=PACK),
                ACT.Square,
            )

        def square_block(name, u, t, b):
            a, t0, planes, j0 = UNITS[u]
            if (name, a) == ("x", 0):
                block = j0 // P + b
                return x0_squares[:, block, t0 + t, :]
            return squares[name, u][:, b, t * P : (t + 1) * P]

        def square_slot(name, u):
            return "square_%s%d" % (name, u)

        squares, roots, h_f32, h_bf16 = {}, {}, {}, {}
        h_codes = sbuf.tile([P, PASSES, S], U32, name="h_codes", align_bytes=64)
        h_scales = sbuf.tile([P, PASSES, S], U8, name="h_scales", align_bytes=64)

        def square(name, u):
            a, t0, planes, j0 = UNITS[u]
            grad = psum.tile([P, PACK // planes, planes * P], F32, name="grad", bufs=GRAD_BANKS)
            rows = slice(t0 * P, (t0 + planes) * P)
            for b in range(PACK // planes):
                cells = slice(j0 + b * P, j0 + (b + 1) * P)
                nc.tensor.matmul_mx(
                    out=grad[:, b, :],
                    lhsT=v_words[:, cells].bitcast(FP8X4),
                    lhsT_scale=cell_scales(cells),
                    rhs=w_codes[name, a][:, rows].bitcast(FP8X4),
                    rhs_scale=w_scales[name, a][:, rows],
                    start=True,
                    stop=True,
                )
            shape = [P, PACK // planes, planes * P]
            if (name, u) in HANDED_ON:
                squares[name, u] = sbuf.tile(shape, F32, name=square_slot(name, u), align_bytes=64)
            else:
                squares[name, u] = sbuf.tile(shape, F32, name="square_" + name, bufs=SQUARE_BUFS)
            nc.scalar.activation(squares[name, u][:], grad[:], ACT.Square)

        def turn(dst, block, start, stop):
            nc.tensor.matmul(dst, block, ident[:], start=start, stop=stop, is_transpose=True)

        totals = {}

        def turn_x_ahead(u):
            totals[u] = psum.tile([P, 1, BANK], F32, name="total_ahead", bufs=SUM_BANKS // 2)
            for b in range(PACK):
                turn(totals[u][:, 0, b * P : (b + 1) * P], square_block("x", u, 0, b), b == 0, False)

        def root(u):
            a, t0, planes, j0 = UNITS[u]
            if u in AHEAD:
                total = totals[u]
                for b in range(PACK):
                    turn(total[:, 0, b * P : (b + 1) * P], square_block("y", u, 0, b), False, b == PACK - 1)
            else:
                name = "total_ahead" if u % 2 == 0 else "total"
                total = psum.tile([P, planes, BANK // planes], F32, name=name, bufs=SUM_BANKS // 2)
                for t in range(planes):
                    for b in range(PACK // planes):
                        for name in ("y", "x"):
                            turn(total[:, t, b * P : (b + 1) * P], square_block(name, u, t, b), name == "y", name == "x")
            roots[u] = sbuf.tile([P, planes, BANK // planes], F32, name="root", bufs=ROOT_BUFS)
            nc.scalar.activation(roots[u][:], total[:], ACT.Sqrt)

        h_f32_slots = {(1, 0): "raw_y0", (1, 1): "raw_x1", (1, 3): square_slot("y", LAST)}

        def flux(u):
            a, t0, planes, j0 = UNITS[u]
            width = BANK // planes
            piece = PIECES[a].index((j0, j0 + width))
            if t0 == 0:
                slot = h_f32_slots.get((a, piece), "h_f32_%d_%d" % (a, piece))
                h_f32[a, piece] = sbuf.tile([P, PACK, width], F32, name=slot, align_bytes=64)
            for t in range(planes):
                nc.vector.tensor_tensor(
                    h_f32[a, piece][:, t0 + t, :],
                    g_rows[a, t0 + t][:].indirect(picks(j0, j0 + width)),
                    roots[u][:, t, :],
                    MULT,
                )

        def round_h(a, piece, slot, shares):
            j0, j1 = PIECES[a][piece]
            h_bf16[a, piece] = sbuf.tile([P, PACK * (j1 - j0)], BF16, name=slot, align_bytes=64)
            for engine, c0, c1 in shares:
                round_copy(
                    engine,
                    h_bf16[a, piece][:, PACK * c0 : PACK * c1].rearrange("p (c i t) -> p c t i", i=LINE, t=PACK),
                    h_f32[a, piece][:, :, c0:c1].rearrange("p t (c i) -> p c t i", i=LINE),
                )

        def quantize_h(a, piece):
            j0, j1 = PIECES[a][piece]
            nc.vector.quantize_mx(
                out=h_codes[:, a, j0:j1].bitcast(FP8X4), scales=h_scales[:, a, j0:j1], in_=h_bf16[a, piece][:]
            )

        accs = {}

        def claim(piece, rings, banks):
            j0, j1 = PIECES[1][piece]
            for u in range(N // P):
                accs[piece, u] = psum.tile([P, j1 - j0], F32, name=rings[u], bufs=banks)

        out_rows = out.rearrange("(u p) j -> p u j", p=P)

        def project(piece, first_engine):
            j0, j1 = PIECES[1][piece]
            width = j1 - j0
            step = BANK if width == BANK else P
            if width >= HALF:
                staged = sbuf.tile([P, N // P, width], F32, name="staged_wide", bufs=2)
            else:
                staged = sbuf.tile([P, N // P, width], F32, name="staged%d" % piece)
            for u in range(N // P):
                acc = accs[piece, u]
                for c0 in range(0, width, step):
                    for a in range(PASSES):
                        nc.tensor.matmul_mx(
                            out=acc[:, c0 : c0 + step],
                            lhsT=w4_codes[:, a, 2 * P * u : 2 * P * (u + 1)].bitcast(FP4X4),
                            lhsT_scale=w4_scale_tile[:, a, P * u : P * (u + 1)],
                            rhs=h_codes[:, a, j0 + c0 : j0 + c0 + step].bitcast(FP8X4),
                            rhs_scale=h_scales[:, a, j0 + c0 : j0 + c0 + step],
                            start=(a == 0),
                            stop=(a == PASSES - 1),
                        )
                if u == 0 and first_engine == "vector":
                    nc.vector.tensor_copy(staged[:, u, :], acc[:])
                else:
                    nc.scalar.copy(staged[:, u, :], acc[:])
            nc.sync.dma_start(out_rows[:, :, j0:j1], staged[:])

        gather_scales(0)
        round_x0(0)
        quantize_x0(0)
        for pair in range(S // HALF):
            gather_words(2 * P * pair, 2 * P * (pair + 1))
        round_x0(1)
        quantize_x0(1)
        gather_scales(1)
        round_w("y", 0, "y_bf16")
        quantize_w("y", 0)
        for pairs in (range(3), range(3, 4)):
            for half in range(2):
                for pair in pairs:
                    square_x0(half, pair, 0, 2)
        round_w("x", 1, "x0_codes1")
        quantize_w("x", 1)
        round_w("y", 1, "y_bf16")
        quantize_w("y", 1)

        def finish(u):
            root(u)
            flux(u)
            if u == PASS0_END:
                round_h(0, 0, square_slot("y", u + LAG), [("vector", 0, BANK)])
            if u == PASS0_END + 1:
                quantize_h(0, 0)

        for first in range(0, LAST - 1, LAG):
            for u in range(first, first + LAG):
                if UNITS[u][0] == 1 and u not in EARLY_DX.values():
                    square("x", u)
                square("y", u)
            if first == 0:
                for u in AHEAD:
                    turn_x_ahead(u)
            if first >= LAG:
                for u in range(first - LAG, first):
                    finish(u)
            if first + 1 in EARLY_DX:
                square("x", EARLY_DX[first + 1])
        for u in (LAST - 1, LAST):
            finish(u - LAG)
            square("x", u)
            square("y", u)
        round_h(1, 0, square_slot("x", LAST - 1), [("scalar", SPLIT, BANK), ("vector", 0, SPLIT)])
        round_h(0, 1, square_slot("y", LAST - 1), [("scalar", 0, BANK)])
        quantize_h(1, 0)
        quantize_h(0, 1)
        finish(LAST - 1)
        root(LAST)

        claim(3, ("total_ahead", "total"), SUM_BANKS // 2)
        claim(0, ("total_ahead", "total"), SUM_BANKS // 2)
        claim(1, ("grad", "grad"), GRAD_BANKS)
        claim(2, ("grad", "grad"), GRAD_BANKS)
        round_h(1, 1, square_slot("y", LAST), [("scalar", 0, HALF)])
        project(0, "scalar")
        round_h(1, 2, square_slot("x", LAST), [("scalar", 0, P)])
        quantize_h(1, 1)
        flux(LAST)
        project(1, "scalar")
        quantize_h(1, 2)
        round_h(1, 3, "h_bf16_last", [("vector", 0, P)])
        project(2, "vector")
        quantize_h(1, 3)
        project(3, "vector")
